import numpy as np
import ml_dtypes


def mxq(x, axis, fmt="e4m3"):
    dtype, down = {"e4m3": (ml_dtypes.float8_e4m3fn, 7), "e5m2": (ml_dtypes.float8_e5m2, 14)}[fmt]
    v = np.moveaxis(np.asarray(x, np.float32).astype(ml_dtypes.bfloat16).astype(np.float64), axis, -1)
    blocks = v.reshape(v.shape[:-1] + (-1, 32))
    amax = np.abs(blocks).max(-1, keepdims=True)
    byte = np.maximum(np.where(amax > 0, np.frexp(amax)[1] - 1 + 127, 0) - down, 1)
    scale = np.exp2(byte - 127.0)
    codes = (blocks / scale).astype(np.float32).astype(dtype).astype(np.float64)
    return np.moveaxis((codes * scale).reshape(v.shape), -1, axis)


WIDE = False


def mx_kscale(k):
    if not WIDE:
        return np.ones(k)
    levels = np.array([10, -10, 5, -5, 0])
    if k % 512:
        return np.exp2(np.random.permutation(np.resize(levels, k // 32))).repeat(32)
    a = np.empty((k // 512, 16))
    for p in range(k // 512):
        a[p, :8] = np.random.permutation(np.resize(levels, 8))
        for g in range(8):
            far = levels[np.abs(levels - a[p, g]) >= 10]
            a[p, g + 8] = far[np.random.randint(len(far))]
    return np.exp2(a.ravel()).repeat(32)


def f64(x):
    return np.asarray(x).astype(np.float64)


def striped(idx):
    return np.tile(np.asarray(idx).reshape(-1, 16).T, (8, 1)).astype(np.uint16)


def unstriped(offs):
    return offs[:16].T.reshape(-1).astype(np.int64)


E2M1 = np.array([0.0, 0.5, 1.0, 1.5, 2.0, 3.0, 4.0, 6.0, -0.0, -0.5, -1.0, -1.5, -2.0, -3.0, -4.0, -6.0])


def pack_weight(w, fmt):
    k, n = w.shape
    w = f64(np.asarray(w, np.float32).astype(ml_dtypes.bfloat16)).reshape(k // 32, 32, n)
    amax = np.abs(w).max(1)
    if fmt == "e4m3":
        byte = np.frexp(amax)[1] - 1 + 127 - 7
    else:
        mant, ex = np.frexp(amax / 6.0)
        byte = np.where(mant > 0.5, ex, ex - 1) + 127
    byte = np.clip(np.where(amax > 0, byte, 1), 1, 254)
    scaled = (w * np.exp2(127.0 - byte)[:, None, :]).reshape(k, n).astype(np.float32)
    by_word = np.ascontiguousarray(scaled.reshape(k // 512, 128, 4, n).transpose(0, 1, 3, 2))
    if fmt == "e4m3":
        words = by_word.astype(ml_dtypes.float8_e4m3fn).view(np.uint8)
    else:
        c = by_word.astype(ml_dtypes.float4_e2m1fn).view(np.uint8) & 0xF
        words = (c[..., 0::2] | (c[..., 1::2] << 4)).reshape(k // 512, 128, 2 * n)
    return np.ascontiguousarray(words), np.ascontiguousarray(byte.astype(np.uint8).reshape(k // 512, 16, n))


def unpack_weight(words, scales, fmt):
    g, _, n = scales.shape
    words = np.ascontiguousarray(words).reshape(g, 128, n, -1)
    if fmt == "e4m3":
        vals = words.view(ml_dtypes.float8_e4m3fn).astype(np.float64)
    else:
        nib = np.empty((g, 128, n, 4), np.uint8)
        nib[..., 0::2] = words & 0xF
        nib[..., 1::2] = words >> 4
        vals = E2M1[nib]
    vals = vals * np.repeat(np.exp2(scales.astype(np.float64) - 127.0), 8, axis=1)[..., None]
    return vals.transpose(0, 1, 3, 2).reshape(g * 512, n)


def sigmoid(v):
    return 1.0 / (1.0 + np.exp(-v))


B, N, T, D, NQ = 1, 512, 2048, 512, 512
DV = 512


def sgn(shape):
    return np.random.uniform(0.5, 2.0, shape) * np.where(np.random.standard_normal(shape) < 0, -1.0, 1.0)


def setup_inputs():
    n = np.random.standard_normal
    idx = np.random.permutation(T)[:B * N]
    s = mx_kscale(D)[:, None]
    u = mx_kscale(N)
    ut = np.ones(T)
    ut[idx] = u
    mid = n((D, T))
    kp = pack_weight((mid + np.abs(n((D, T)))) / s, "e4m3")
    cp = pack_weight((mid - np.abs(n((D, T)))) / s, "e4m3")
    return {
        "qT": (n((B, D, NQ)) * s * (1.00 / np.sqrt(D))).astype(np.float32),
        "k_words": kp[0],
        "k_scales": kp[1],
        "c_words": cp[0],
        "c_scales": cp[1],
        "vT": (n((DV, T)) / ut).astype(np.float32),
        "th": (14 + 2 * n((B, 1, NQ))).astype(np.float32),
        "us": (sgn((B, N, 1)) * u[:, None]).astype(np.float32),
        "offs": striped(idx),
    }


def reference(qT, k_words, k_scales, c_words, c_scales, vT, th, us, offs):
    idx = unstriped(offs)
    pick = lambda x, which: x[:, which].reshape(x.shape[0], B, -1).transpose(1, 0, 2)
    k = unpack_weight(k_words, k_scales, "e4m3")
    kg = pick(k, idx)
    c = unpack_weight(c_words, c_scales, "e4m3")
    cg = pick(c, idx)
    hiq = mxq(np.maximum(f64(qT), 0.0), 1, "e4m3")
    loq = mxq(np.minimum(f64(qT), 0.0), 1, "e4m3")
    a = (kg.transpose(0, 2, 1) @ hiq) + (cg.transpose(0, 2, 1) @ loq)
    y = sigmoid(a - f64(th)) * f64(us)
    wq = mxq(y, 1, "e4m3")
    o = wq.transpose(0, 2, 1) @ mxq(pick(f64(vT), idx).transpose(0, 2, 1), 1, "e4m3")
    return o

@@ -1,0 +1,176 @@
+from contextlib import ExitStack
+
+import concourse.mybir as mybir
+
+F32 = mybir.dt.float32
+BF16 = mybir.dt.bfloat16
+I32 = mybir.dt.int32
+U32 = mybir.dt.uint32
+U16 = mybir.dt.uint16
+U8 = mybir.dt.uint8
+FP8X4 = mybir.dt.float8_e4m3fn_x4
+ACT = mybir.ActivationFunctionType
+ALU = mybir.AluOpType
+
+P = 128
+PACK = 4
+SLOTS, PAGES, D, NQ, DV = 512, 2048, 512, 512, 512
+QB = NQ // P
+EB = DV // P
+C_PLANE = 4
+ROW_BYTES = 4 * PAGES
+
+FLOPS = 2 * SLOTS * NQ * (2 * D + DV)
+
+
+def tile_attend_at_quest_topk_kernel(tc, qT, k_words, k_scales, c_words, c_scales, vT, th, us, offs, out):
+    nc = tc.nc
+    with ExitStack() as ctx:
+        held = ctx.enter_context(tc.tile_pool(name="held", bufs=1))
+        big = ctx.enter_context(tc.tile_pool(name="big", bufs=1))
+        psum = ctx.enter_context(tc.psum_pool(name="psum", bufs=1))
+
+        offsets = held.tile([P, SLOTS // 16], U16, name="offsets")
+        nc.sync.dma_start(offsets[:], offs)
+
+        ks_all = held.tile([P, PAGES], U8, name="ks_all")
+        cs_all = held.tile([P, PAGES], U8, name="cs_all")
+        ident = held.tile([P, P], F32, name="ident")
+        zeros = big.tile([P, 6 * PAGES + 8], F32, name="zeros", offset=0)
+        nc.vector.memset(cs_all[:].bitcast(I32), 0)
+        nc.gpsimd.memset(zeros[:, 0:P], 0.0)
+        nc.gpsimd.memset(ks_all[:].bitcast(I32), 0)
+        nc.gpsimd.affine_select(out=ident[:], in_=zeros[:, 0:P], compare_op=ALU.not_equal, fill=1.0, base=0,
+                                pattern=[[-1, P]], channel_multiplier=1)
+        th_rows = held.tile([P, P], F32, name="th_rows")
+        us_col = big.tile([P, PACK], F32, name="us_col", offset=6 * ROW_BYTES)
+        nc.vector.memset(th_rows[:], 0.0)
+
+        q_raw = held.tile([P, PACK, NQ], F32, name="q_raw")
+        nc.sync.dma_start(out=q_raw[:], in_=qT[0].rearrange("(p j) q -> p j q", j=PACK))
+        for r in range(4):
+            nc.scalar.dma_start(out=cs_all[C_PLANE + r:P:32, :].bitcast(I32), in_=c_scales[0, r:16:4, :].bitcast(I32))
+        for r in range(4):
+            queue = nc.gpsimd if r < 2 else nc.sync
+            queue.dma_start(out=ks_all[r:P:32, :].bitcast(I32), in_=k_scales[0, r:16:4, :].bitcast(I32))
+        nc.gpsimd.dma_start(out=th_rows[0:QB, :], in_=th[0, 0].rearrange("(c p) -> c p", p=P))
+        warm = held.tile([P, 1], F32, name="warm")
+        nc.scalar.activation(out=warm[:], in_=ident[:, 0:1], func=ACT.Sigmoid)
+        cw_all = big.tile([P, PAGES], I32, name="cw_all", offset=0)
+        nc.sync.dma_start(out=cw_all[:], in_=c_words[0].rearrange("p n t -> p (n t)").bitcast(I32))
+        kw_all = big.tile([P, PAGES], I32, name="kw_all", offset=ROW_BYTES)
+        nc.sync.dma_start(out=kw_all[:], in_=k_words[0].rearrange("p n t -> p (n t)").bitcast(I32))
+        nc.sync.dma_start(out=us_col[:], in_=us[0].rearrange("(p t) o -> p (t o)", t=PACK))
+        v_all = []
+        for a in range(EB):
+            v_tile = big.tile([P, PAGES], F32, name=f"v_all{a}", offset=(2 + a) * ROW_BYTES)
+            nc.sync.dma_start(out=v_tile[:], in_=vT[a * P:(a + 1) * P, :])
+            v_all.append(v_tile)
+
+        cs_g = held.tile([P, SLOTS], U8, name="cs_g", align_bytes=64)
+        nc.vector.tensor_copy(out=cs_g[:], in_=cs_all[:].indirect(offsets[:]))
+        ks_g = held.tile([P, SLOTS], U8, name="ks_g", align_bytes=64)
+        nc.vector.tensor_copy(out=ks_g[:], in_=ks_all[:].indirect(offsets[:]))
+        cw_g = held.tile([P, SLOTS], U32, name="cw_g", align_bytes=64)
+        nc.vector.tensor_copy(out=cw_g[:], in_=cw_all[:].bitcast(U32).indirect(offsets[:]))
+
+        q_b = held.tile([P, NQ, PACK], BF16, name="q_b", align_bytes=64)
+        hi_b = held.tile([P, NQ, PACK], BF16, name="hi_b", align_bytes=64)
+        lo_b = held.tile([P, NQ, PACK], BF16, name="lo_b", align_bytes=64)
+        lo_codes = held.tile([P, NQ], U32, name="lo_codes", align_bytes=64)
+        lo_scales = held.tile([P, NQ], U8, name="lo_scales", align_bytes=64)
+        hi_codes = held.tile([P, NQ], U32, name="hi_codes", align_bytes=64)
+        hi_scales = held.tile([P, NQ], U8, name="hi_scales", align_bytes=64)
+        halves = [slice(h * NQ // 2, (h + 1) * NQ // 2) for h in range(2)]
+        for cols in halves:
+            nc.scalar.copy(out=q_b[:, cols, :].rearrange("p (g i) j -> p g j i", i=4),
+                           in_=q_raw[:, :, cols].rearrange("p j (g i) -> p g j i", i=4))
+        for cols in halves:
+            nc.vector.tensor_scalar_min(out=lo_b[:, cols, :], in0=q_b[:, cols, :], scalar1=0.0)
+        for cols in halves:
+            nc.vector.quantize_mx(out=lo_codes[:, cols].bitcast(FP8X4), scales=lo_scales[:, cols],
+                                  in_=lo_b[:, cols, :].rearrange("p q j -> p (q j)"))
+        for cols in halves:
+            nc.scalar.activation(out=hi_b[:, cols, :], in_=q_b[:, cols, :], func=ACT.Relu)
+        nc.vector.quantize_mx(out=hi_codes[:, halves[0]].bitcast(FP8X4), scales=hi_scales[:, halves[0]],
+                              in_=hi_b[:, halves[0], :].rearrange("p q j -> p (q j)"))
+        kw_g = held.tile([P, SLOTS], U32, name="kw_g", align_bytes=64)
+        nc.vector.tensor_copy(out=kw_g[:], in_=kw_all[:].bitcast(U32).indirect(offsets[:]))
+        nc.vector.quantize_mx(out=hi_codes[:, halves[1]].bitcast(FP8X4), scales=hi_scales[:, halves[1]],
+                              in_=hi_b[:, halves[1], :].rearrange("p q j -> p (q j)"))
+
+        th_ps = psum.tile([P, P], F32, name="th_ps", tag="turn", bufs=2)
+        nc.tensor.transpose(th_ps[:], th_rows[:], ident[:])
+        neg_th = held.tile([P, QB], F32, name="neg_th")
+        nc.scalar.activation(out=neg_th[:], in_=th_ps[:, 0:QB], func=ACT.Copy, scale=-1.0)
+
+        scores = [psum.tile([P, SLOTS], F32, name=f"score{c}", tag="acc", bufs=4) for c in range(QB)]
+        for c in range(QB):
+            cols = slice(c * P, (c + 1) * P)
+            nc.tensor.matmul_mx(out=scores[c][:], lhsT=lo_codes[:, cols].bitcast(FP8X4), lhsT_scale=lo_scales[:, cols],
+                                rhs=cw_g[:].bitcast(FP8X4), rhs_scale=cs_g[C_PLANE:P, :], start=True, stop=False)
+        for c in range(QB):
+            cols = slice(c * P, (c + 1) * P)
+            nc.tensor.matmul_mx(out=scores[c][:], lhsT=hi_codes[:, cols].bitcast(FP8X4), lhsT_scale=hi_scales[:, cols],
+                                rhs=kw_g[:].bitcast(FP8X4), rhs_scale=ks_g[:], start=False, stop=True)
+
+        us_wide = us_col[:].unsqueeze(1).to_broadcast([P, P, PACK])
+        y_codes, y_scales, y_bf = [], [], []
+
+        def gate(c):
+            sig = held.tile([P, PACK, P], F32, name=f"sig{c}")
+            nc.scalar.activation(out=sig[:], in_=scores[c][:].rearrange("q (s t) -> q t s", t=PACK),
+                                 func=ACT.Sigmoid, bias=neg_th[:, c:c + 1])
+            turned = psum.tile([P, PACK, P], F32, name=f"y_ps{c}", tag="turn", bufs=2)
+            for t in range(PACK):
+                nc.tensor.transpose(turned[:, t, :], sig[:, t, :], ident[:])
+            y_b = big.tile([P, P, PACK], BF16, name=f"y_b{c}", offset=2 * ROW_BYTES + c * 1024, align_bytes=64)
+            nc.vector.tensor_tensor(out=y_b[:], in0=turned[:].rearrange("p t q -> p q t"), in1=us_wide, op=ALU.mult)
+            y_bf.append(y_b)
+
+        def quantise_gate(c):
+            codes = held.tile([P, P], U32, name=f"y_codes{c}", align_bytes=64)
+            scales = held.tile([P, P], U8, name=f"y_scales{c}", align_bytes=64)
+            nc.vector.quantize_mx(out=codes[:].bitcast(FP8X4), scales=scales[:],
+                                  in_=y_bf[c][:].rearrange("p q t -> p (q t)"))
+            y_codes.append(codes)
+            y_scales.append(scales)
+
+        out_rows = out[0].rearrange("(c p) e -> p c e", p=P)
+        v_pairs = []
+
+        def gather_values(a):
+            v_g = held.tile([P, SLOTS], BF16, name=f"v_g{a}")
+            nc.vector.tensor_copy(out=v_g[:], in_=v_all[a][:].indirect(offsets[:]))
+            pairs = v_g[:].bitcast(F32)
+            v_ps = psum.tile([P, 2, P], F32, name=f"v_ps{a}", tag="vturn", bufs=2)
+            for u in range(2):
+                nc.tensor.transpose(v_ps[:, u, :], pairs[:, u:SLOTS // 2:2], ident[:])
+            v_b = held.tile([P, P, 2], F32, name=f"v_b{a}", align_bytes=64)
+            nc.scalar.copy(out=v_b[:], in_=v_ps[:].rearrange("p u e -> p e u"))
+            v_pairs.append(v_b)
+
+        def finish(a):
+            home = (2 + min(a + 1, EB - 1)) * ROW_BYTES + (a % 2) * 1024
+            v_codes = big.tile([P, P], U32, name=f"v_codes{a}", offset=home, align_bytes=64)
+            v_scales = big.tile([P, P], U8, name=f"v_scales{a}", offset=home + 512, align_bytes=64)
+            nc.vector.quantize_mx(out=v_codes[:].bitcast(FP8X4), scales=v_scales[:],
+                                  in_=v_pairs[a][:].rearrange("p e u -> p (e u)").bitcast(BF16))
+            acc = psum.tile([P, QB, P], F32, name=f"out_ps{a}", tag="acc", bufs=4)
+            for c in range(QB):
+                nc.tensor.matmul_mx(out=acc[:, c, :], lhsT=y_codes[c][:].bitcast(FP8X4), lhsT_scale=y_scales[c][:],
+                                    rhs=v_codes[:].bitcast(FP8X4), rhs_scale=v_scales[:], start=True, stop=True)
+            result = held.tile([P, QB, P], F32, name=f"result{a}")
+            nc.scalar.copy(out=result[:], in_=acc[:])
+            nc.sync.dma_start(out=out_rows[:, :, a * P:(a + 1) * P], in_=result[:])
+
+        gather_values(0)
+        for c in range(QB):
+            gate(c)
+            if c > 0:
+                quantise_gate(c - 1)
+        quantise_gate(QB - 1)
+        for a in range(1, EB):
+            gather_values(a)
+            finish(a - 1)
+        finish(EB - 1)

@@ -19,6 +19,12 @@ QB = NQ // P
 EB = DV // P
 C_PLANE = 4
 ROW_BYTES = 4 * PAGES
+KB = 1024
+CW_HOME, CS_HOME, LO_HOME, KW_HOME = 0, 10 * KB, 10 * KB, 14 * KB
+V_HOME = (22 * KB, 46 * KB, 30 * KB, 38 * KB)
+US_HOME, TH_HOME, HI_HOME, KS_HOME = 54 * KB, 55 * KB, 56 * KB, 60 * KB
+VG_HOME = (HI_HOME + 2 * KB, TH_HOME, US_HOME + 32 - KB, V_HOME[2] + 2 * KB)
+BANK = 2048
 
 FLOPS = 2 * SLOTS * NQ * (2 * D + DV)
 
@@ -33,85 +39,88 @@ def tile_attend_at_quest_topk_kernel(tc, qT, k_words, k_scales, c_words, c_scale
         offsets = held.tile([P, SLOTS // 16], U16, name="offsets")
         nc.sync.dma_start(offsets[:], offs)
 
-        ks_all = held.tile([P, PAGES], U8, name="ks_all")
-        cs_all = held.tile([P, PAGES], U8, name="cs_all")
         ident = held.tile([P, P], F32, name="ident")
-        zeros = big.tile([P, 6 * PAGES + 8], F32, name="zeros", offset=0)
-        nc.vector.memset(cs_all[:].bitcast(I32), 0)
-        nc.gpsimd.memset(zeros[:, 0:P], 0.0)
-        nc.gpsimd.memset(ks_all[:].bitcast(I32), 0)
-        nc.gpsimd.affine_select(out=ident[:], in_=zeros[:, 0:P], compare_op=ALU.not_equal, fill=1.0, base=0,
-                                pattern=[[-1, P]], channel_multiplier=1)
         th_rows = held.tile([P, P], F32, name="th_rows")
-        us_col = big.tile([P, PACK], F32, name="us_col", offset=6 * ROW_BYTES)
+        us_col = big.tile([P, PACK], F32, name="us_col", offset=US_HOME)
+        warm = held.tile([P, 1], F32, name="warm")
+        cs_all = big.tile([P, PAGES], U8, name="cs_all", offset=CS_HOME)
+        ks_all = big.tile([P, PAGES], U8, name="ks_all", offset=KS_HOME)
+        zeros_a = big.tile([P, P // 2], F32, name="zeros_a", offset=CW_HOME)
+        zeros_b = big.tile([P, (US_HOME - KW_HOME) // 4], F32, name="zeros_b", offset=KW_HOME)
+        nc.vector.memset(warm[:], 0.0)
+        nc.scalar.activation(out=warm[:], in_=warm[:], func=ACT.Sigmoid)
+        nc.gpsimd.memset(zeros_a[:], 0.0)
+        nc.gpsimd.memset(zeros_b[:, 0:P // 2], 0.0)
+        nc.gpsimd.memset(cs_all[:].bitcast(I32), 0)
         nc.vector.memset(th_rows[:], 0.0)
+        nc.gpsimd.affine_select(out=ident[:, 0:P // 2], in_=zeros_a[:], compare_op=ALU.not_equal, fill=1.0, base=0,
+                                pattern=[[-1, P // 2]], channel_multiplier=1)
+        nc.gpsimd.memset(ks_all[:].bitcast(I32), 0)
+        nc.gpsimd.affine_select(out=ident[:, P // 2:P], in_=zeros_b[:, 0:P // 2], compare_op=ALU.not_equal, fill=1.0,
+                                base=-(P // 2), pattern=[[-1, P // 2]], channel_multiplier=1)
 
         q_raw = held.tile([P, PACK, NQ], F32, name="q_raw")
         nc.sync.dma_start(out=q_raw[:], in_=qT[0].rearrange("(p j) q -> p j q", j=PACK))
+        nc.sync.dma_start(out=us_col[:], in_=us[0].rearrange("(p t) o -> p (t o)", t=PACK))
+        nc.sync.dma_start(out=th_rows[0:QB, :], in_=th[0, 0].rearrange("(c p) -> c p", p=P))
         for r in range(4):
             nc.scalar.dma_start(out=cs_all[C_PLANE + r:P:32, :].bitcast(I32), in_=c_scales[0, r:16:4, :].bitcast(I32))
-        for r in range(4):
-            queue = nc.gpsimd if r < 2 else nc.sync
-            queue.dma_start(out=ks_all[r:P:32, :].bitcast(I32), in_=k_scales[0, r:16:4, :].bitcast(I32))
-        nc.gpsimd.dma_start(out=th_rows[0:QB, :], in_=th[0, 0].rearrange("(c p) -> c p", p=P))
-        warm = held.tile([P, 1], F32, name="warm")
-        nc.scalar.activation(out=warm[:], in_=ident[:, 0:1], func=ACT.Sigmoid)
-        cw_all = big.tile([P, PAGES], I32, name="cw_all", offset=0)
+        cw_all = big.tile([P, PAGES], I32, name="cw_all", offset=CW_HOME)
         nc.sync.dma_start(out=cw_all[:], in_=c_words[0].rearrange("p n t -> p (n t)").bitcast(I32))
-        kw_all = big.tile([P, PAGES], I32, name="kw_all", offset=ROW_BYTES)
-        nc.sync.dma_start(out=kw_all[:], in_=k_words[0].rearrange("p n t -> p (n t)").bitcast(I32))
-        nc.sync.dma_start(out=us_col[:], in_=us[0].rearrange("(p t) o -> p (t o)", t=PACK))
-        v_all = []
-        for a in range(EB):
-            v_tile = big.tile([P, PAGES], F32, name=f"v_all{a}", offset=(2 + a) * ROW_BYTES)
-            nc.sync.dma_start(out=v_tile[:], in_=vT[a * P:(a + 1) * P, :])
-            v_all.append(v_tile)
+        for r in range(4):
+            nc.sync.dma_start(out=ks_all[r:P:32, :].bitcast(I32), in_=k_scales[0, r:16:4, :].bitcast(I32))
 
         cs_g = held.tile([P, SLOTS], U8, name="cs_g", align_bytes=64)
         nc.vector.tensor_copy(out=cs_g[:], in_=cs_all[:].indirect(offsets[:]))
-        ks_g = held.tile([P, SLOTS], U8, name="ks_g", align_bytes=64)
-        nc.vector.tensor_copy(out=ks_g[:], in_=ks_all[:].indirect(offsets[:]))
-        cw_g = held.tile([P, SLOTS], U32, name="cw_g", align_bytes=64)
-        nc.vector.tensor_copy(out=cw_g[:], in_=cw_all[:].bitcast(U32).indirect(offsets[:]))
+        kw_all = big.tile([P, PAGES], I32, name="kw_all", offset=KW_HOME)
+        nc.sync.dma_start(out=kw_all[:], in_=k_words[0].rearrange("p n t -> p (n t)").bitcast(I32))
+        v_all = []
+        for a in range(EB):
+            v_tile = big.tile([P, PAGES], F32, name=f"v_all{a}", offset=V_HOME[a])
+            nc.sync.dma_start(out=v_tile[:], in_=vT[a * P:(a + 1) * P, :])
+            v_all.append(v_tile)
 
-        q_b = held.tile([P, NQ, PACK], BF16, name="q_b", align_bytes=64)
-        hi_b = held.tile([P, NQ, PACK], BF16, name="hi_b", align_bytes=64)
-        lo_b = held.tile([P, NQ, PACK], BF16, name="lo_b", align_bytes=64)
+        hi_b = [big.tile([P, NQ // 2, PACK], BF16, name=f"hi_b{h}", offset=HI_HOME + h * 2048, align_bytes=64) for h in range(2)]
+        lo_b = big.tile([P, NQ, PACK], BF16, name="lo_b", offset=LO_HOME, align_bytes=64)
         lo_codes = held.tile([P, NQ], U32, name="lo_codes", align_bytes=64)
         lo_scales = held.tile([P, NQ], U8, name="lo_scales", align_bytes=64)
-        hi_codes = held.tile([P, NQ], U32, name="hi_codes", align_bytes=64)
-        hi_scales = held.tile([P, NQ], U8, name="hi_scales", align_bytes=64)
         halves = [slice(h * NQ // 2, (h + 1) * NQ // 2) for h in range(2)]
-        for cols in halves:
-            nc.scalar.copy(out=q_b[:, cols, :].rearrange("p (g i) j -> p g j i", i=4),
-                           in_=q_raw[:, :, cols].rearrange("p j (g i) -> p g j i", i=4))
-        for cols in halves:
-            nc.vector.tensor_scalar_min(out=lo_b[:, cols, :], in0=q_b[:, cols, :], scalar1=0.0)
+        for h, cols in enumerate(halves):
+            q_src = q_raw[:, :, cols].rearrange("p j (g i) -> p g j i", i=4)
+            nc.scalar.activation(out=hi_b[h][:].rearrange("p (g i) j -> p g j i", i=4), in_=q_src, func=ACT.Relu)
+            nc.vector.tensor_scalar_min(out=lo_b[:, cols, :].rearrange("p (g i) j -> p g j i", i=4), in0=q_src, scalar1=0.0)
+
         for cols in halves:
             nc.vector.quantize_mx(out=lo_codes[:, cols].bitcast(FP8X4), scales=lo_scales[:, cols],
                                   in_=lo_b[:, cols, :].rearrange("p q j -> p (q j)"))
-        for cols in halves:
-            nc.scalar.activation(out=hi_b[:, cols, :], in_=q_b[:, cols, :], func=ACT.Relu)
-        nc.vector.quantize_mx(out=hi_codes[:, halves[0]].bitcast(FP8X4), scales=hi_scales[:, halves[0]],
-                              in_=hi_b[:, halves[0], :].rearrange("p q j -> p (q j)"))
-        kw_g = held.tile([P, SLOTS], U32, name="kw_g", align_bytes=64)
+        cw_g = big.tile([P, SLOTS], U32, name="cw_g", offset=LO_HOME, align_bytes=64)
+        nc.vector.tensor_copy(out=cw_g[:], in_=cw_all[:].bitcast(U32).indirect(offsets[:]))
+        ks_g = big.tile([P, SLOTS], U8, name="ks_g", offset=CW_HOME, align_bytes=64)
+        nc.vector.tensor_copy(out=ks_g[:], in_=ks_all[:].indirect(offsets[:]))
+        hi_codes = [big.tile([P, NQ // 2], U32, name="hi_codes0", offset=KS_HOME, align_bytes=64)]
+        hi_scales = [held.tile([P, NQ // 2], U8, name="hi_scales0", align_bytes=64)]
+        nc.vector.quantize_mx(out=hi_codes[0][:].bitcast(FP8X4), scales=hi_scales[0][:],
+                              in_=hi_b[0][:].rearrange("p q j -> p (q j)"))
+        kw_g = big.tile([P, SLOTS], U32, name="kw_g", offset=HI_HOME, align_bytes=64)
         nc.vector.tensor_copy(out=kw_g[:], in_=kw_all[:].bitcast(U32).indirect(offsets[:]))
-        nc.vector.quantize_mx(out=hi_codes[:, halves[1]].bitcast(FP8X4), scales=hi_scales[:, halves[1]],
-                              in_=hi_b[:, halves[1], :].rearrange("p q j -> p (q j)"))
+        hi_codes.append(big.tile([P, NQ // 2], U32, name="hi_codes1", offset=KW_HOME, align_bytes=64))
+        hi_scales.append(big.tile([P, NQ // 2], U8, name="hi_scales1", offset=KW_HOME + 1024, align_bytes=64))
+        nc.vector.quantize_mx(out=hi_codes[1][:].bitcast(FP8X4), scales=hi_scales[1][:],
+                              in_=hi_b[1][:].rearrange("p q j -> p (q j)"))
 
-        th_ps = psum.tile([P, P], F32, name="th_ps", tag="turn", bufs=2)
+        th_ps = psum.tile([P, P], F32, name="th_ps", offset=7 * BANK)
         nc.tensor.transpose(th_ps[:], th_rows[:], ident[:])
-        neg_th = held.tile([P, QB], F32, name="neg_th")
+        neg_th = big.tile([P, QB], F32, name="neg_th", offset=TH_HOME)
         nc.scalar.activation(out=neg_th[:], in_=th_ps[:, 0:QB], func=ACT.Copy, scale=-1.0)
 
-        scores = [psum.tile([P, SLOTS], F32, name=f"score{c}", tag="acc", bufs=4) for c in range(QB)]
+        scores = [psum.tile([P, SLOTS], F32, name=f"score{c}", offset=c * BANK) for c in range(QB)]
         for c in range(QB):
             cols = slice(c * P, (c + 1) * P)
             nc.tensor.matmul_mx(out=scores[c][:], lhsT=lo_codes[:, cols].bitcast(FP8X4), lhsT_scale=lo_scales[:, cols],
                                 rhs=cw_g[:].bitcast(FP8X4), rhs_scale=cs_g[C_PLANE:P, :], start=True, stop=False)
         for c in range(QB):
-            cols = slice(c * P, (c + 1) * P)
-            nc.tensor.matmul_mx(out=scores[c][:], lhsT=hi_codes[:, cols].bitcast(FP8X4), lhsT_scale=hi_scales[:, cols],
+            cols = slice(c % 2 * P, (c % 2 + 1) * P)
+            nc.tensor.matmul_mx(out=scores[c][:], lhsT=hi_codes[c // 2][:, cols].bitcast(FP8X4), lhsT_scale=hi_scales[c // 2][:, cols],
                                 rhs=kw_g[:].bitcast(FP8X4), rhs_scale=ks_g[:], start=False, stop=True)
 
         us_wide = us_col[:].unsqueeze(1).to_broadcast([P, P, PACK])
@@ -121,10 +130,10 @@ def tile_attend_at_quest_topk_kernel(tc, qT, k_words, k_scales, c_words, c_scale
             sig = held.tile([P, PACK, P], F32, name=f"sig{c}")
             nc.scalar.activation(out=sig[:], in_=scores[c][:].rearrange("q (s t) -> q t s", t=PACK),
                                  func=ACT.Sigmoid, bias=neg_th[:, c:c + 1])
-            turned = psum.tile([P, PACK, P], F32, name=f"y_ps{c}", tag="turn", bufs=2)
+            turned = psum.tile([P, PACK, P], F32, name=f"y_ps{c}", offset=(4 + c % 2) * BANK)
             for t in range(PACK):
                 nc.tensor.transpose(turned[:, t, :], sig[:, t, :], ident[:])
-            y_b = big.tile([P, P, PACK], BF16, name=f"y_b{c}", offset=2 * ROW_BYTES + c * 1024, align_bytes=64)
+            y_b = big.tile([P, P, PACK], BF16, name=f"y_b{c}", offset=V_HOME[0] + c * 1024, align_bytes=64)
             nc.vector.tensor_tensor(out=y_b[:], in0=turned[:].rearrange("p t q -> p q t"), in1=us_wide, op=ALU.mult)
             y_bf.append(y_b)
 
@@ -137,13 +146,16 @@ def tile_attend_at_quest_topk_kernel(tc, qT, k_words, k_scales, c_words, c_scale
             y_scales.append(scales)
 
         out_rows = out[0].rearrange("(c p) e -> p c e", p=P)
-        v_pairs = []
+        v_gathered, v_pairs = [], []
 
         def gather_values(a):
-            v_g = held.tile([P, SLOTS], BF16, name=f"v_g{a}")
+            v_g = big.tile([P, SLOTS], BF16, name=f"v_g{a}", offset=VG_HOME[a])
             nc.vector.tensor_copy(out=v_g[:], in_=v_all[a][:].indirect(offsets[:]))
-            pairs = v_g[:].bitcast(F32)
-            v_ps = psum.tile([P, 2, P], F32, name=f"v_ps{a}", tag="vturn", bufs=2)
+            v_gathered.append(v_g)
+
+        def turn_values(a):
+            pairs = v_gathered[a][:].bitcast(F32)
+            v_ps = psum.tile([P, 2, P], F32, name=f"v_ps{a}", offset=a * BANK)
             for u in range(2):
                 nc.tensor.transpose(v_ps[:, u, :], pairs[:, u:SLOTS // 2:2], ident[:])
             v_b = held.tile([P, P, 2], F32, name=f"v_b{a}", align_bytes=64)
@@ -151,12 +163,12 @@ def tile_attend_at_quest_topk_kernel(tc, qT, k_words, k_scales, c_words, c_scale
             v_pairs.append(v_b)
 
         def finish(a):
-            home = (2 + min(a + 1, EB - 1)) * ROW_BYTES + (a % 2) * 1024
+            home = V_HOME[min(a + 1, EB - 1)] + (a % 2) * 1024
             v_codes = big.tile([P, P], U32, name=f"v_codes{a}", offset=home, align_bytes=64)
             v_scales = big.tile([P, P], U8, name=f"v_scales{a}", offset=home + 512, align_bytes=64)
             nc.vector.quantize_mx(out=v_codes[:].bitcast(FP8X4), scales=v_scales[:],
                                   in_=v_pairs[a][:].rearrange("p e u -> p (e u)").bitcast(BF16))
-            acc = psum.tile([P, QB, P], F32, name=f"out_ps{a}", tag="acc", bufs=4)
+            acc = psum.tile([P, QB, P], F32, name=f"out_ps{a}", offset=(6, 7, 4, 5)[a] * BANK)
             for c in range(QB):
                 nc.tensor.matmul_mx(out=acc[:, c, :], lhsT=y_codes[c][:].bitcast(FP8X4), lhsT_scale=y_scales[c][:],
                                     rhs=v_codes[:].bitcast(FP8X4), rhs_scale=v_scales[:], start=True, stop=True)
@@ -170,7 +182,14 @@ def tile_attend_at_quest_topk_kernel(tc, qT, k_words, k_scales, c_words, c_scale
             if c > 0:
                 quantise_gate(c - 1)
         quantise_gate(QB - 1)
-        for a in range(1, EB):
-            gather_values(a)
-            finish(a - 1)
-        finish(EB - 1)
+        turn_values(0)
+        gather_values(1)
+        turn_values(1)
+        finish(0)
+        gather_values(2)
+        turn_values(2)
+        finish(1)
+        gather_values(3)
+        turn_values(3)
+        finish(2)
+        finish(3)

@@ -17,13 +17,16 @@ PACK = 4
 SLOTS, PAGES, D, NQ, DV = 512, 2048, 512, 512, 512
 QB = NQ // P
 EB = DV // P
+HALF = NQ // 2
 C_PLANE = 4
-ROW_BYTES = 4 * PAGES
+
 KB = 1024
-CW_HOME, CS_HOME, LO_HOME, KW_HOME = 0, 10 * KB, 10 * KB, 14 * KB
-V_HOME = (22 * KB, 46 * KB, 30 * KB, 38 * KB)
-US_HOME, TH_HOME, HI_HOME, KS_HOME = 54 * KB, 55 * KB, 56 * KB, 60 * KB
-VG_HOME = (HI_HOME + 2 * KB, TH_HOME, US_HOME + 32 - KB, V_HOME[2] + 2 * KB)
+Q_HOME, CS_HOME, KS_HOME, QBF_HOME, HI_HOME, TH_HOME = 0, 8 * KB, 12 * KB, 14 * KB, 18 * KB, 22 * KB
+CW_HOME, KW_HOME = 23 * KB, 31 * KB
+V_HOME = (39 * KB, 63 * KB, 47 * KB, 55 * KB)
+US_HOME = 71 * KB
+LATE_END = US_HOME + 32
+VG_HOME = (HI_HOME + 2 * KB, TH_HOME, LATE_END - KB, V_HOME[2] + 2 * KB)
 BANK = 2048
 
 FLOPS = 2 * SLOTS * NQ * (2 * D + DV)
@@ -33,84 +36,90 @@ def tile_attend_at_quest_topk_kernel(tc, qT, k_words, k_scales, c_words, c_scale
     nc = tc.nc
     with ExitStack() as ctx:
         held = ctx.enter_context(tc.tile_pool(name="held", bufs=1))
-        big = ctx.enter_context(tc.tile_pool(name="big", bufs=1))
+        placed = ctx.enter_context(tc.tile_pool(name="placed", bufs=1))
         psum = ctx.enter_context(tc.psum_pool(name="psum", bufs=1))
+
+        def quantise(codes, scales, values):
+            nc.vector.quantize_mx(out=codes.bitcast(FP8X4), scales=scales, in_=values)
 
         offsets = held.tile([P, SLOTS // 16], U16, name="offsets")
         nc.sync.dma_start(offsets[:], offs)
 
         ident = held.tile([P, P], F32, name="ident")
         th_rows = held.tile([P, P], F32, name="th_rows")
-        us_col = big.tile([P, PACK], F32, name="us_col", offset=US_HOME)
         warm = held.tile([P, 1], F32, name="warm")
-        cs_all = big.tile([P, PAGES], U8, name="cs_all", offset=CS_HOME)
-        ks_all = big.tile([P, PAGES], U8, name="ks_all", offset=KS_HOME)
-        zeros_a = big.tile([P, P // 2], F32, name="zeros_a", offset=CW_HOME)
-        zeros_b = big.tile([P, (US_HOME - KW_HOME) // 4], F32, name="zeros_b", offset=KW_HOME)
+        cs_all = placed.tile([P, PAGES], U8, name="cs_all", offset=CS_HOME)
+        ks_all = placed.tile([P, PAGES], U8, name="ks_all", offset=KS_HOME)
+        zeros_a = placed.tile([P, P // 2], F32, name="zeros_a", offset=Q_HOME)
+        zeros_b = placed.tile([P, (LATE_END - CW_HOME) // 4], F32, name="zeros_b", offset=CW_HOME)
         nc.vector.memset(warm[:], 0.0)
         nc.scalar.activation(out=warm[:], in_=warm[:], func=ACT.Sigmoid)
+        nc.vector.memset(th_rows[:], 0.0)
         nc.gpsimd.memset(zeros_a[:], 0.0)
         nc.gpsimd.memset(zeros_b[:, 0:P // 2], 0.0)
         nc.gpsimd.memset(cs_all[:].bitcast(I32), 0)
-        nc.vector.memset(th_rows[:], 0.0)
         nc.gpsimd.affine_select(out=ident[:, 0:P // 2], in_=zeros_a[:], compare_op=ALU.not_equal, fill=1.0, base=0,
                                 pattern=[[-1, P // 2]], channel_multiplier=1)
         nc.gpsimd.memset(ks_all[:].bitcast(I32), 0)
         nc.gpsimd.affine_select(out=ident[:, P // 2:P], in_=zeros_b[:, 0:P // 2], compare_op=ALU.not_equal, fill=1.0,
                                 base=-(P // 2), pattern=[[-1, P // 2]], channel_multiplier=1)
 
-        q_raw = held.tile([P, PACK, NQ], F32, name="q_raw")
-        nc.sync.dma_start(out=q_raw[:], in_=qT[0].rearrange("(p j) q -> p j q", j=PACK))
-        nc.sync.dma_start(out=us_col[:], in_=us[0].rearrange("(p t) o -> p (t o)", t=PACK))
         nc.sync.dma_start(out=th_rows[0:QB, :], in_=th[0, 0].rearrange("(c p) -> c p", p=P))
         for r in range(4):
-            nc.scalar.dma_start(out=cs_all[C_PLANE + r:P:32, :].bitcast(I32), in_=c_scales[0, r:16:4, :].bitcast(I32))
-        cw_all = big.tile([P, PAGES], I32, name="cw_all", offset=CW_HOME)
-        nc.sync.dma_start(out=cw_all[:], in_=c_words[0].rearrange("p n t -> p (n t)").bitcast(I32))
+            nc.sync.dma_start(out=cs_all[C_PLANE + r:P:32, :].bitcast(I32), in_=c_scales[0, r:16:4, :].bitcast(I32))
+        q_raw = placed.tile([P, PACK, NQ], F32, name="q_raw", offset=Q_HOME)
+        nc.sync.dma_start(out=q_raw[:], in_=qT[0].rearrange("(p j) q -> p j q", j=PACK))
         for r in range(4):
             nc.sync.dma_start(out=ks_all[r:P:32, :].bitcast(I32), in_=k_scales[0, r:16:4, :].bitcast(I32))
-
-        cs_g = held.tile([P, SLOTS], U8, name="cs_g", align_bytes=64)
-        nc.vector.tensor_copy(out=cs_g[:], in_=cs_all[:].indirect(offsets[:]))
-        kw_all = big.tile([P, PAGES], I32, name="kw_all", offset=KW_HOME)
+        cw_all = placed.tile([P, PAGES], I32, name="cw_all", offset=CW_HOME)
+        nc.sync.dma_start(out=cw_all[:], in_=c_words[0].rearrange("p n t -> p (n t)").bitcast(I32))
+        kw_all = placed.tile([P, PAGES], I32, name="kw_all", offset=KW_HOME)
         nc.sync.dma_start(out=kw_all[:], in_=k_words[0].rearrange("p n t -> p (n t)").bitcast(I32))
+        us_col = placed.tile([P, PACK], F32, name="us_col", offset=US_HOME)
+        nc.sync.dma_start(out=us_col[:], in_=us[0].rearrange("(p t) o -> p (t o)", t=PACK))
         v_all = []
         for a in range(EB):
-            v_tile = big.tile([P, PAGES], F32, name=f"v_all{a}", offset=V_HOME[a])
+            v_tile = placed.tile([P, PAGES], F32, name=f"v_all{a}", offset=V_HOME[a])
             nc.sync.dma_start(out=v_tile[:], in_=vT[a * P:(a + 1) * P, :])
             v_all.append(v_tile)
 
-        hi_b = [big.tile([P, NQ // 2, PACK], BF16, name=f"hi_b{h}", offset=HI_HOME + h * 2048, align_bytes=64) for h in range(2)]
-        lo_b = big.tile([P, NQ, PACK], BF16, name="lo_b", offset=LO_HOME, align_bytes=64)
+        cs_g = held.tile([P, SLOTS], U8, name="cs_g", align_bytes=64)
+        nc.vector.tensor_copy(out=cs_g[:], in_=cs_all[:].indirect(offsets[:]))
+        ks_g = placed.tile([P, SLOTS], U8, name="ks_g", offset=CS_HOME, align_bytes=64)
+        nc.vector.tensor_copy(out=ks_g[:], in_=ks_all[:].indirect(offsets[:]))
+
+        q_bf, lo_bf, hi_bf = [], [], []
+        for h in range(2):
+            rounded = placed.tile([P, HALF, PACK], BF16, name=f"q_bf{h}", offset=QBF_HOME + h * 2 * KB)
+            nc.scalar.copy(out=rounded[:], in_=q_raw[:, :, h * HALF:(h + 1) * HALF].rearrange("p j q -> p q j"))
+            q_bf.append(rounded[:].rearrange("p q j -> p (q j)"))
+        for h in range(2):
+            positive = placed.tile([P, HALF * PACK], BF16, name=f"hi_bf{h}", offset=HI_HOME + h * 2 * KB, align_bytes=64)
+            nc.scalar.activation(out=positive[:], in_=q_bf[h], func=ACT.Relu)
+            hi_bf.append(positive)
+
         lo_codes = held.tile([P, NQ], U32, name="lo_codes", align_bytes=64)
         lo_scales = held.tile([P, NQ], U8, name="lo_scales", align_bytes=64)
-        halves = [slice(h * NQ // 2, (h + 1) * NQ // 2) for h in range(2)]
-        for h, cols in enumerate(halves):
-            q_src = q_raw[:, :, cols].rearrange("p j (g i) -> p g j i", i=4)
-            nc.scalar.activation(out=hi_b[h][:].rearrange("p (g i) j -> p g j i", i=4), in_=q_src, func=ACT.Relu)
-            nc.vector.tensor_scalar_min(out=lo_b[:, cols, :].rearrange("p (g i) j -> p g j i", i=4), in0=q_src, scalar1=0.0)
-
-        for cols in halves:
-            nc.vector.quantize_mx(out=lo_codes[:, cols].bitcast(FP8X4), scales=lo_scales[:, cols],
-                                  in_=lo_b[:, cols, :].rearrange("p q j -> p (q j)"))
-        cw_g = big.tile([P, SLOTS], U32, name="cw_g", offset=LO_HOME, align_bytes=64)
+        lo_bf.append(placed.tile([P, HALF * PACK], BF16, name="lo_bf0", offset=KS_HOME, align_bytes=64))
+        nc.vector.tensor_scalar_min(out=lo_bf[0][:], in0=q_bf[0], scalar1=0.0)
+        quantise(lo_codes[:, 0:HALF], lo_scales[:, 0:HALF], lo_bf[0][:])
+        cw_g = placed.tile([P, SLOTS], U32, name="cw_g", offset=KS_HOME, align_bytes=64)
         nc.vector.tensor_copy(out=cw_g[:], in_=cw_all[:].bitcast(U32).indirect(offsets[:]))
-        ks_g = big.tile([P, SLOTS], U8, name="ks_g", offset=CW_HOME, align_bytes=64)
-        nc.vector.tensor_copy(out=ks_g[:], in_=ks_all[:].indirect(offsets[:]))
-        hi_codes = [big.tile([P, NQ // 2], U32, name="hi_codes0", offset=KS_HOME, align_bytes=64)]
-        hi_scales = [held.tile([P, NQ // 2], U8, name="hi_scales0", align_bytes=64)]
-        nc.vector.quantize_mx(out=hi_codes[0][:].bitcast(FP8X4), scales=hi_scales[0][:],
-                              in_=hi_b[0][:].rearrange("p q j -> p (q j)"))
-        kw_g = big.tile([P, SLOTS], U32, name="kw_g", offset=HI_HOME, align_bytes=64)
+        lo_bf.append(placed.tile([P, HALF * PACK], BF16, name="lo_bf1", offset=CW_HOME, align_bytes=64))
+        nc.vector.tensor_scalar_min(out=lo_bf[1][:], in0=q_bf[1], scalar1=0.0)
+        hi_codes = [placed.tile([P, HALF], U32, name="hi_codes0", offset=CW_HOME + 2 * KB, align_bytes=64)]
+        hi_scales = [held.tile([P, HALF], U8, name="hi_scales0", align_bytes=64)]
+        quantise(hi_codes[0][:], hi_scales[0][:], hi_bf[0][:])
+        quantise(lo_codes[:, HALF:NQ], lo_scales[:, HALF:NQ], lo_bf[1][:])
+        kw_g = placed.tile([P, SLOTS], U32, name="kw_g", offset=CW_HOME, align_bytes=64)
         nc.vector.tensor_copy(out=kw_g[:], in_=kw_all[:].bitcast(U32).indirect(offsets[:]))
-        hi_codes.append(big.tile([P, NQ // 2], U32, name="hi_codes1", offset=KW_HOME, align_bytes=64))
-        hi_scales.append(big.tile([P, NQ // 2], U8, name="hi_scales1", offset=KW_HOME + 1024, align_bytes=64))
-        nc.vector.quantize_mx(out=hi_codes[1][:].bitcast(FP8X4), scales=hi_scales[1][:],
-                              in_=hi_b[1][:].rearrange("p q j -> p (q j)"))
+        hi_codes.append(placed.tile([P, HALF], U32, name="hi_codes1", offset=KW_HOME, align_bytes=64))
+        hi_scales.append(held.tile([P, HALF], U8, name="hi_scales1", align_bytes=64))
+        quantise(hi_codes[1][:], hi_scales[1][:], hi_bf[1][:])
 
         th_ps = psum.tile([P, P], F32, name="th_ps", offset=7 * BANK)
         nc.tensor.transpose(th_ps[:], th_rows[:], ident[:])
-        neg_th = big.tile([P, QB], F32, name="neg_th", offset=TH_HOME)
+        neg_th = placed.tile([P, QB], F32, name="neg_th", offset=TH_HOME)
         nc.scalar.activation(out=neg_th[:], in_=th_ps[:, 0:QB], func=ACT.Copy, scale=-1.0)
 
         scores = [psum.tile([P, SLOTS], F32, name=f"score{c}", offset=c * BANK) for c in range(QB)]
@@ -120,11 +129,13 @@ def tile_attend_at_quest_topk_kernel(tc, qT, k_words, k_scales, c_words, c_scale
                                 rhs=cw_g[:].bitcast(FP8X4), rhs_scale=cs_g[C_PLANE:P, :], start=True, stop=False)
         for c in range(QB):
             cols = slice(c % 2 * P, (c % 2 + 1) * P)
-            nc.tensor.matmul_mx(out=scores[c][:], lhsT=hi_codes[c // 2][:, cols].bitcast(FP8X4), lhsT_scale=hi_scales[c // 2][:, cols],
+            nc.tensor.matmul_mx(out=scores[c][:], lhsT=hi_codes[c // 2][:, cols].bitcast(FP8X4),
+                                lhsT_scale=hi_scales[c // 2][:, cols],
                                 rhs=kw_g[:].bitcast(FP8X4), rhs_scale=ks_g[:], start=False, stop=True)
 
         us_wide = us_col[:].unsqueeze(1).to_broadcast([P, P, PACK])
-        y_codes, y_scales, y_bf = [], [], []
+        out_rows = out[0].rearrange("(c p) e -> p c e", p=P)
+        y_bf, y_codes, y_scales, v_gathered, v_pairs = [], [], [], [], []
 
         def gate(c):
             sig = held.tile([P, PACK, P], F32, name=f"sig{c}")
@@ -133,23 +144,18 @@ def tile_attend_at_quest_topk_kernel(tc, qT, k_words, k_scales, c_words, c_scale
             turned = psum.tile([P, PACK, P], F32, name=f"y_ps{c}", offset=(4 + c % 2) * BANK)
             for t in range(PACK):
                 nc.tensor.transpose(turned[:, t, :], sig[:, t, :], ident[:])
-            y_b = big.tile([P, P, PACK], BF16, name=f"y_b{c}", offset=V_HOME[0] + c * 1024, align_bytes=64)
-            nc.vector.tensor_tensor(out=y_b[:], in0=turned[:].rearrange("p t q -> p q t"), in1=us_wide, op=ALU.mult)
-            y_bf.append(y_b)
+            if c % 2 == 0:
+                y_bf.append(placed.tile([P, HALF, PACK], BF16, name=f"y_bf{c // 2}", offset=V_HOME[0] + c * KB, align_bytes=64))
+            nc.vector.tensor_tensor(out=y_bf[c // 2][:, c % 2 * P:(c % 2 + 1) * P, :],
+                                    in0=turned[:].rearrange("p t q -> p q t"), in1=us_wide, op=ALU.mult)
 
-        def quantise_gate(c):
-            codes = held.tile([P, P], U32, name=f"y_codes{c}", align_bytes=64)
-            scales = held.tile([P, P], U8, name=f"y_scales{c}", align_bytes=64)
-            nc.vector.quantize_mx(out=codes[:].bitcast(FP8X4), scales=scales[:],
-                                  in_=y_bf[c][:].rearrange("p q t -> p (q t)"))
-            y_codes.append(codes)
-            y_scales.append(scales)
-
-        out_rows = out[0].rearrange("(c p) e -> p c e", p=P)
-        v_gathered, v_pairs = [], []
+        def quantise_gates(h):
+            y_codes.append(held.tile([P, HALF], U32, name=f"y_codes{h}", align_bytes=64))
+            y_scales.append(held.tile([P, HALF], U8, name=f"y_scales{h}", align_bytes=64))
+            quantise(y_codes[h][:], y_scales[h][:], y_bf[h][:].rearrange("p q t -> p (q t)"))
 
         def gather_values(a):
-            v_g = big.tile([P, SLOTS], BF16, name=f"v_g{a}", offset=VG_HOME[a])
+            v_g = placed.tile([P, SLOTS], BF16, name=f"v_g{a}", offset=VG_HOME[a])
             nc.vector.tensor_copy(out=v_g[:], in_=v_all[a][:].indirect(offsets[:]))
             v_gathered.append(v_g)
 
@@ -162,34 +168,43 @@ def tile_attend_at_quest_topk_kernel(tc, qT, k_words, k_scales, c_words, c_scale
             nc.scalar.copy(out=v_b[:], in_=v_ps[:].rearrange("p u e -> p e u"))
             v_pairs.append(v_b)
 
-        def finish(a):
-            home = V_HOME[min(a + 1, EB - 1)] + (a % 2) * 1024
-            v_codes = big.tile([P, P], U32, name=f"v_codes{a}", offset=home, align_bytes=64)
-            v_scales = big.tile([P, P], U8, name=f"v_scales{a}", offset=home + 512, align_bytes=64)
-            nc.vector.quantize_mx(out=v_codes[:].bitcast(FP8X4), scales=v_scales[:],
-                                  in_=v_pairs[a][:].rearrange("p e u -> p (e u)").bitcast(BF16))
-            acc = psum.tile([P, QB, P], F32, name=f"out_ps{a}", offset=(6, 7, 4, 5)[a] * BANK)
-            for c in range(QB):
-                nc.tensor.matmul_mx(out=acc[:, c, :], lhsT=y_codes[c][:].bitcast(FP8X4), lhsT_scale=y_scales[c][:],
+        def quantise_values(a):
+            home = V_HOME[min(a + 1, EB - 1)] + (a % 2) * KB
+            v_codes = placed.tile([P, P], U32, name=f"v_codes{a}", offset=home, align_bytes=64)
+            v_scales = placed.tile([P, P], U8, name=f"v_scales{a}", offset=home + 512, align_bytes=64)
+            quantise(v_codes[:], v_scales[:], v_pairs[a][:].rearrange("p e u -> p (e u)").bitcast(BF16))
+            return v_codes, v_scales
+
+        def multiply(a, operand, blocks, bank, copy, queue):
+            v_codes, v_scales = operand
+            name = f"{a}_{blocks[0]}"
+            acc = psum.tile([P, len(blocks), P], F32, name="out_ps" + name, offset=bank * BANK)
+            for i, c in enumerate(blocks):
+                cols = slice(c % 2 * P, (c % 2 + 1) * P)
+                nc.tensor.matmul_mx(out=acc[:, i, :], lhsT=y_codes[c // 2][:, cols].bitcast(FP8X4),
+                                    lhsT_scale=y_scales[c // 2][:, cols],
                                     rhs=v_codes[:].bitcast(FP8X4), rhs_scale=v_scales[:], start=True, stop=True)
-            result = held.tile([P, QB, P], F32, name=f"result{a}")
-            nc.scalar.copy(out=result[:], in_=acc[:])
-            nc.sync.dma_start(out=out_rows[:, :, a * P:(a + 1) * P], in_=result[:])
+            result = held.tile([P, len(blocks), P], F32, name="result" + name)
+            copy(out=result[:], in_=acc[:])
+            queue.dma_start(out=out_rows[:, blocks[0]:blocks[-1] + 1, a * P:(a + 1) * P], in_=result[:])
 
         gather_values(0)
-        for c in range(QB):
-            gate(c)
-            if c > 0:
-                quantise_gate(c - 1)
-        quantise_gate(QB - 1)
+        gate(0)
+        gate(1)
+        gate(2)
+        quantise_gates(0)
+        gate(3)
         turn_values(0)
         gather_values(1)
+        quantise_gates(1)
         turn_values(1)
-        finish(0)
+        multiply(0, quantise_values(0), [0, 1, 2, 3], 6, nc.scalar.copy, nc.sync)
         gather_values(2)
         turn_values(2)
-        finish(1)
+        multiply(1, quantise_values(1), [0, 1, 2, 3], 7, nc.scalar.copy, nc.sync)
         gather_values(3)
         turn_values(3)
-        finish(2)
-        finish(3)
+        multiply(2, quantise_values(2), [0, 1, 2, 3], 4, nc.scalar.copy, nc.sync)
+        last = quantise_values(3)
+        multiply(3, last, [0, 1], 5, nc.scalar.copy, nc.scalar)
+        multiply(3, last, [2, 3], 0, nc.vector.tensor_copy, nc.sync)

@@ -21,12 +21,13 @@ HALF = NQ // 2
 C_PLANE = 4
 
 KB = 1024
-Q_HOME, CS_HOME, KS_HOME, QBF_HOME, HI_HOME, TH_HOME = 0, 8 * KB, 12 * KB, 14 * KB, 18 * KB, 22 * KB
+Q_HOME, CS_HOME, KS_HOME, HI_HOME, TH_HOME = 0, 8 * KB, 12 * KB, 18 * KB, 22 * KB
 CW_HOME, KW_HOME = 23 * KB, 31 * KB
 V_HOME = (39 * KB, 63 * KB, 47 * KB, 55 * KB)
 US_HOME = 71 * KB
 LATE_END = US_HOME + 32
-VG_HOME = (HI_HOME + 2 * KB, TH_HOME, LATE_END - KB, V_HOME[2] + 2 * KB)
+Y_HOME = (V_HOME[1] + 2 * KB, V_HOME[2] + 2 * KB)
+VG_HOME = (HI_HOME + 2 * KB, V_HOME[0], TH_HOME, Y_HOME[1])
 BANK = 2048
 
 FLOPS = 2 * SLOTS * NQ * (2 * D + DV)
@@ -50,25 +51,24 @@ def tile_attend_at_quest_topk_kernel(tc, qT, k_words, k_scales, c_words, c_scale
         warm = held.tile([P, 1], F32, name="warm")
         cs_all = placed.tile([P, PAGES], U8, name="cs_all", offset=CS_HOME)
         ks_all = placed.tile([P, PAGES], U8, name="ks_all", offset=KS_HOME)
-        zeros_a = placed.tile([P, P // 2], F32, name="zeros_a", offset=Q_HOME)
+        zeros_a = placed.tile([P, P], F32, name="zeros_a", offset=Q_HOME)
         zeros_b = placed.tile([P, (LATE_END - CW_HOME) // 4], F32, name="zeros_b", offset=CW_HOME)
         nc.vector.memset(warm[:], 0.0)
         nc.scalar.activation(out=warm[:], in_=warm[:], func=ACT.Sigmoid)
-        nc.vector.memset(th_rows[:], 0.0)
         nc.gpsimd.memset(zeros_a[:], 0.0)
-        nc.gpsimd.memset(zeros_b[:, 0:P // 2], 0.0)
-        nc.gpsimd.memset(cs_all[:].bitcast(I32), 0)
-        nc.gpsimd.affine_select(out=ident[:, 0:P // 2], in_=zeros_a[:], compare_op=ALU.not_equal, fill=1.0, base=0,
-                                pattern=[[-1, P // 2]], channel_multiplier=1)
+        nc.gpsimd.memset(zeros_b[:, 0:P], 0.0)
+        nc.vector.memset(cs_all[:].bitcast(I32), 0)
+        nc.vector.tensor_copy(out=th_rows[:], in_=zeros_a[:])
         nc.gpsimd.memset(ks_all[:].bitcast(I32), 0)
-        nc.gpsimd.affine_select(out=ident[:, P // 2:P], in_=zeros_b[:, 0:P // 2], compare_op=ALU.not_equal, fill=1.0,
-                                base=-(P // 2), pattern=[[-1, P // 2]], channel_multiplier=1)
+        nc.gpsimd.affine_select(out=ident[:], in_=zeros_b[:, 0:P], compare_op=ALU.not_equal, fill=1.0, base=0,
+                                pattern=[[-1, P]], channel_multiplier=1)
 
-        nc.sync.dma_start(out=th_rows[0:QB, :], in_=th[0, 0].rearrange("(c p) -> c p", p=P))
         for r in range(4):
-            nc.sync.dma_start(out=cs_all[C_PLANE + r:P:32, :].bitcast(I32), in_=c_scales[0, r:16:4, :].bitcast(I32))
+            queue = nc.sync if r < 2 else nc.scalar
+            queue.dma_start(out=cs_all[C_PLANE + r:P:32, :].bitcast(I32), in_=c_scales[0, r:16:4, :].bitcast(I32))
         q_raw = placed.tile([P, PACK, NQ], F32, name="q_raw", offset=Q_HOME)
         nc.sync.dma_start(out=q_raw[:], in_=qT[0].rearrange("(p j) q -> p j q", j=PACK))
+        nc.sync.dma_start(out=th_rows[0:QB, :], in_=th[0, 0].rearrange("(c p) -> c p", p=P))
         for r in range(4):
             nc.sync.dma_start(out=ks_all[r:P:32, :].bitcast(I32), in_=k_scales[0, r:16:4, :].bitcast(I32))
         cw_all = placed.tile([P, PAGES], I32, name="cw_all", offset=CW_HOME)
@@ -85,37 +85,33 @@ def tile_attend_at_quest_topk_kernel(tc, qT, k_words, k_scales, c_words, c_scale
 
         cs_g = held.tile([P, SLOTS], U8, name="cs_g", align_bytes=64)
         nc.vector.tensor_copy(out=cs_g[:], in_=cs_all[:].indirect(offsets[:]))
-        ks_g = placed.tile([P, SLOTS], U8, name="ks_g", offset=CS_HOME, align_bytes=64)
+
+        lo_bf = placed.tile([P, NQ, PACK], BF16, name="lo_bf", offset=CS_HOME, align_bytes=64)
+        hi_bf = []
+        for h in range(2):
+            cols = slice(h * HALF, (h + 1) * HALF)
+            source = q_raw[:, :, cols].rearrange("p j (g i) -> p g j i", i=4)
+            positive = placed.tile([P, HALF, PACK], BF16, name=f"hi_bf{h}", offset=HI_HOME + h * 2 * KB, align_bytes=64)
+            nc.scalar.activation(out=positive[:].rearrange("p (g i) j -> p g j i", i=4), in_=source, func=ACT.Relu)
+            nc.vector.tensor_scalar_min(out=lo_bf[:, cols, :].rearrange("p (g i) j -> p g j i", i=4), in0=source,
+                                        scalar1=0.0)
+            hi_bf.append(positive[:].rearrange("p q j -> p (q j)"))
+
+        ks_g = held.tile([P, SLOTS], U8, name="ks_g", align_bytes=64)
         nc.vector.tensor_copy(out=ks_g[:], in_=ks_all[:].indirect(offsets[:]))
-
-        q_bf, lo_bf, hi_bf = [], [], []
-        for h in range(2):
-            rounded = placed.tile([P, HALF, PACK], BF16, name=f"q_bf{h}", offset=QBF_HOME + h * 2 * KB)
-            nc.scalar.copy(out=rounded[:], in_=q_raw[:, :, h * HALF:(h + 1) * HALF].rearrange("p j q -> p q j"))
-            q_bf.append(rounded[:].rearrange("p q j -> p (q j)"))
-        for h in range(2):
-            positive = placed.tile([P, HALF * PACK], BF16, name=f"hi_bf{h}", offset=HI_HOME + h * 2 * KB, align_bytes=64)
-            nc.scalar.activation(out=positive[:], in_=q_bf[h], func=ACT.Relu)
-            hi_bf.append(positive)
-
         lo_codes = held.tile([P, NQ], U32, name="lo_codes", align_bytes=64)
         lo_scales = held.tile([P, NQ], U8, name="lo_scales", align_bytes=64)
-        lo_bf.append(placed.tile([P, HALF * PACK], BF16, name="lo_bf0", offset=KS_HOME, align_bytes=64))
-        nc.vector.tensor_scalar_min(out=lo_bf[0][:], in0=q_bf[0], scalar1=0.0)
-        quantise(lo_codes[:, 0:HALF], lo_scales[:, 0:HALF], lo_bf[0][:])
-        cw_g = placed.tile([P, SLOTS], U32, name="cw_g", offset=KS_HOME, align_bytes=64)
+        quantise(lo_codes[:], lo_scales[:], lo_bf[:].rearrange("p q j -> p (q j)"))
+        cw_g = placed.tile([P, SLOTS], U32, name="cw_g", offset=CS_HOME, align_bytes=64)
         nc.vector.tensor_copy(out=cw_g[:], in_=cw_all[:].bitcast(U32).indirect(offsets[:]))
-        lo_bf.append(placed.tile([P, HALF * PACK], BF16, name="lo_bf1", offset=CW_HOME, align_bytes=64))
-        nc.vector.tensor_scalar_min(out=lo_bf[1][:], in0=q_bf[1], scalar1=0.0)
-        hi_codes = [placed.tile([P, HALF], U32, name="hi_codes0", offset=CW_HOME + 2 * KB, align_bytes=64)]
-        hi_scales = [held.tile([P, HALF], U8, name="hi_scales0", align_bytes=64)]
-        quantise(hi_codes[0][:], hi_scales[0][:], hi_bf[0][:])
-        quantise(lo_codes[:, HALF:NQ], lo_scales[:, HALF:NQ], lo_bf[1][:])
-        kw_g = placed.tile([P, SLOTS], U32, name="kw_g", offset=CW_HOME, align_bytes=64)
+        hi_codes = [placed.tile([P, HALF], U32, name="hi_codes0", offset=KS_HOME, align_bytes=64)]
+        hi_scales = [placed.tile([P, HALF], U8, name="hi_scales0", offset=CW_HOME, align_bytes=64)]
+        quantise(hi_codes[0][:], hi_scales[0][:], hi_bf[0])
+        kw_g = placed.tile([P, SLOTS], U32, name="kw_g", offset=HI_HOME, align_bytes=64)
         nc.vector.tensor_copy(out=kw_g[:], in_=kw_all[:].bitcast(U32).indirect(offsets[:]))
         hi_codes.append(placed.tile([P, HALF], U32, name="hi_codes1", offset=KW_HOME, align_bytes=64))
         hi_scales.append(held.tile([P, HALF], U8, name="hi_scales1", align_bytes=64))
-        quantise(hi_codes[1][:], hi_scales[1][:], hi_bf[1][:])
+        quantise(hi_codes[1][:], hi_scales[1][:], hi_bf[1])
 
         th_ps = psum.tile([P, P], F32, name="th_ps", offset=7 * BANK)
         nc.tensor.transpose(th_ps[:], th_rows[:], ident[:])
@@ -123,31 +119,54 @@ def tile_attend_at_quest_topk_kernel(tc, qT, k_words, k_scales, c_words, c_scale
         nc.scalar.activation(out=neg_th[:], in_=th_ps[:, 0:QB], func=ACT.Copy, scale=-1.0)
 
         scores = [psum.tile([P, SLOTS], F32, name=f"score{c}", offset=c * BANK) for c in range(QB)]
-        for c in range(QB):
+
+        def score_low(c):
             cols = slice(c * P, (c + 1) * P)
             nc.tensor.matmul_mx(out=scores[c][:], lhsT=lo_codes[:, cols].bitcast(FP8X4), lhsT_scale=lo_scales[:, cols],
                                 rhs=cw_g[:].bitcast(FP8X4), rhs_scale=cs_g[C_PLANE:P, :], start=True, stop=False)
-        for c in range(QB):
+
+        def score_high(c):
             cols = slice(c % 2 * P, (c % 2 + 1) * P)
             nc.tensor.matmul_mx(out=scores[c][:], lhsT=hi_codes[c // 2][:, cols].bitcast(FP8X4),
                                 lhsT_scale=hi_scales[c // 2][:, cols],
                                 rhs=kw_g[:].bitcast(FP8X4), rhs_scale=ks_g[:], start=False, stop=True)
 
-        us_wide = us_col[:].unsqueeze(1).to_broadcast([P, P, PACK])
+        for c in range(QB - 1):
+            score_low(c)
+        for c in range(QB - 1):
+            score_high(c)
+        score_low(QB - 1)
+        score_high(QB - 1)
+
         out_rows = out[0].rearrange("(c p) e -> p c e", p=P)
-        y_bf, y_codes, y_scales, v_gathered, v_pairs = [], [], [], [], []
+        y_bf = [placed.tile([P, HALF, PACK], BF16, name=f"y_bf{h}", offset=Y_HOME[h], align_bytes=64) for h in range(2)]
+        y_codes, y_scales, v_gathered, v_pairs = [], [], [], []
 
         def gate(c):
             sig = held.tile([P, PACK, P], F32, name=f"sig{c}")
             nc.scalar.activation(out=sig[:], in_=scores[c][:].rearrange("q (s t) -> q t s", t=PACK),
                                  func=ACT.Sigmoid, bias=neg_th[:, c:c + 1])
-            turned = psum.tile([P, PACK, P], F32, name=f"y_ps{c}", offset=(4 + c % 2) * BANK)
+            return sig
+
+        def scale_on_vector(c):
+            sig = gate(c)
+            turned = psum.tile([P, PACK, P], F32, name=f"y_ps{c}", offset=(4 + c) * BANK)
             for t in range(PACK):
                 nc.tensor.transpose(turned[:, t, :], sig[:, t, :], ident[:])
-            if c % 2 == 0:
-                y_bf.append(placed.tile([P, HALF, PACK], BF16, name=f"y_bf{c // 2}", offset=V_HOME[0] + c * KB, align_bytes=64))
-            nc.vector.tensor_tensor(out=y_bf[c // 2][:, c % 2 * P:(c % 2 + 1) * P, :],
-                                    in0=turned[:].rearrange("p t q -> p q t"), in1=us_wide, op=ALU.mult)
+            nc.vector.tensor_tensor(out=y_bf[0][:, c * P:(c + 1) * P, :], in0=turned[:].rearrange("p t q -> p q t"),
+                                    in1=us_col[:].unsqueeze(1).to_broadcast([P, P, PACK]), op=ALU.mult)
+
+        def scale_on_scalar():
+            turned = [psum.tile([P, 2, HALF], F32, name=f"y_ps{2 + u}", offset=(6 + u) * BANK) for u in range(2)]
+            for i in range(2):
+                sig = gate(2 + i)
+                for t in range(PACK):
+                    nc.tensor.transpose(turned[t // 2][:, t % 2, i * P:(i + 1) * P], sig[:, t, :], ident[:])
+            planes = held.tile([P, PACK, HALF], BF16, name="y_planes")
+            for t in range(PACK):
+                nc.scalar.activation(out=planes[:, t, :], in_=turned[t // 2][:, t % 2, :], func=ACT.Copy,
+                                     scale=us_col[:, t:t + 1])
+            return planes
 
         def quantise_gates(h):
             y_codes.append(held.tile([P, HALF], U32, name=f"y_codes{h}", align_bytes=64))
@@ -161,7 +180,7 @@ def tile_attend_at_quest_topk_kernel(tc, qT, k_words, k_scales, c_words, c_scale
 
         def turn_values(a):
             pairs = v_gathered[a][:].bitcast(F32)
-            v_ps = psum.tile([P, 2, P], F32, name=f"v_ps{a}", offset=a * BANK)
+            v_ps = psum.tile([P, 2, P], F32, name=f"v_ps{a}", offset=(0, 6, 7, 3)[a] * BANK)
             for u in range(2):
                 nc.tensor.transpose(v_ps[:, u, :], pairs[:, u:SLOTS // 2:2], ident[:])
             v_b = held.tile([P, P, 2], F32, name=f"v_b{a}", align_bytes=64)
@@ -189,22 +208,24 @@ def tile_attend_at_quest_topk_kernel(tc, qT, k_words, k_scales, c_words, c_scale
             queue.dma_start(out=out_rows[:, blocks[0]:blocks[-1] + 1, a * P:(a + 1) * P], in_=result[:])
 
         gather_values(0)
-        gate(0)
-        gate(1)
-        gate(2)
-        quantise_gates(0)
-        gate(3)
-        turn_values(0)
         gather_values(1)
-        quantise_gates(1)
-        turn_values(1)
-        multiply(0, quantise_values(0), [0, 1, 2, 3], 6, nc.scalar.copy, nc.sync)
+        scale_on_vector(0)
+        scale_on_vector(1)
+        y_planes = scale_on_scalar()
+        quantise_gates(0)
         gather_values(2)
+        nc.vector.tensor_copy(out=y_bf[1][:], in_=y_planes[:].rearrange("p t q -> p q t"))
+        turn_values(0)
+        turn_values(1)
         turn_values(2)
-        multiply(1, quantise_values(1), [0, 1, 2, 3], 7, nc.scalar.copy, nc.sync)
+        first = quantise_values(0)
+        quantise_gates(1)
+        second = quantise_values(1)
+        multiply(0, first, [0, 1, 2, 3], 4, nc.scalar.copy, nc.sync)
+        multiply(1, second, [0, 1, 2, 3], 5, nc.scalar.copy, nc.sync)
         gather_values(3)
         turn_values(3)
-        multiply(2, quantise_values(2), [0, 1, 2, 3], 4, nc.scalar.copy, nc.sync)
+        multiply(2, quantise_values(2), [0, 1, 2, 3], 1, nc.scalar.copy, nc.sync)
         last = quantise_values(3)
-        multiply(3, last, [0, 1], 5, nc.scalar.copy, nc.scalar)
+        multiply(3, last, [0, 1], 2, nc.scalar.copy, nc.scalar)
         multiply(3, last, [2, 3], 0, nc.vector.tensor_copy, nc.sync)

@@ -18,6 +18,8 @@ SLOTS, PAGES, D, NQ, DV = 512, 2048, 512, 512, 512
 QB = NQ // P
 EB = DV // P
 HALF = NQ // 2
+RUN = 4
+SCALE_ROWS, QUADRANT = 16, 32
 C_PLANE = 4
 
 KB = 1024
@@ -26,9 +28,15 @@ CW_HOME, KW_HOME = 23 * KB, 31 * KB
 V_HOME = (39 * KB, 63 * KB, 47 * KB, 55 * KB)
 US_HOME = 71 * KB
 LATE_END = US_HOME + 32
-Y_HOME = (V_HOME[1] + 2 * KB, V_HOME[2] + 2 * KB)
+Y_HOME = (V_HOME[2] + 2 * KB, V_HOME[2] + 4 * KB)
 VG_HOME = (HI_HOME + 2 * KB, V_HOME[0], TH_HOME, Y_HOME[1])
+
 BANK = 2048
+GATE_BANK = QB
+TH_BANK = 7
+V_TURN_BANK = (0, 6, 7, 3)
+OUT_BANK = (4, 5, 1)
+LAST_OUT_BANK = (2, 0)
 
 FLOPS = 2 * SLOTS * NQ * (2 * D + DV)
 
@@ -65,12 +73,14 @@ def tile_attend_at_quest_topk_kernel(tc, qT, k_words, k_scales, c_words, c_scale
 
         for r in range(4):
             queue = nc.sync if r < 2 else nc.scalar
-            queue.dma_start(out=cs_all[C_PLANE + r:P:32, :].bitcast(I32), in_=c_scales[0, r:16:4, :].bitcast(I32))
+            queue.dma_start(out=cs_all[C_PLANE + r:P:QUADRANT, :].bitcast(I32),
+                            in_=c_scales[0, r:SCALE_ROWS:4, :].bitcast(I32))
         q_raw = placed.tile([P, PACK, NQ], F32, name="q_raw", offset=Q_HOME)
         nc.sync.dma_start(out=q_raw[:], in_=qT[0].rearrange("(p j) q -> p j q", j=PACK))
         nc.sync.dma_start(out=th_rows[0:QB, :], in_=th[0, 0].rearrange("(c p) -> c p", p=P))
         for r in range(4):
-            nc.sync.dma_start(out=ks_all[r:P:32, :].bitcast(I32), in_=k_scales[0, r:16:4, :].bitcast(I32))
+            nc.sync.dma_start(out=ks_all[r:P:QUADRANT, :].bitcast(I32),
+                              in_=k_scales[0, r:SCALE_ROWS:4, :].bitcast(I32))
         cw_all = placed.tile([P, PAGES], I32, name="cw_all", offset=CW_HOME)
         nc.sync.dma_start(out=cw_all[:], in_=c_words[0].rearrange("p n t -> p (n t)").bitcast(I32))
         kw_all = placed.tile([P, PAGES], I32, name="kw_all", offset=KW_HOME)
@@ -90,10 +100,10 @@ def tile_attend_at_quest_topk_kernel(tc, qT, k_words, k_scales, c_words, c_scale
         hi_bf = []
         for h in range(2):
             cols = slice(h * HALF, (h + 1) * HALF)
-            source = q_raw[:, :, cols].rearrange("p j (g i) -> p g j i", i=4)
+            source = q_raw[:, :, cols].rearrange("p j (g i) -> p g j i", i=RUN)
             positive = placed.tile([P, HALF, PACK], BF16, name=f"hi_bf{h}", offset=HI_HOME + h * 2 * KB, align_bytes=64)
-            nc.scalar.activation(out=positive[:].rearrange("p (g i) j -> p g j i", i=4), in_=source, func=ACT.Relu)
-            nc.vector.tensor_scalar_min(out=lo_bf[:, cols, :].rearrange("p (g i) j -> p g j i", i=4), in0=source,
+            nc.scalar.activation(out=positive[:].rearrange("p (g i) j -> p g j i", i=RUN), in_=source, func=ACT.Relu)
+            nc.vector.tensor_scalar_min(out=lo_bf[:, cols, :].rearrange("p (g i) j -> p g j i", i=RUN), in0=source,
                                         scalar1=0.0)
             hi_bf.append(positive[:].rearrange("p q j -> p (q j)"))
 
@@ -113,7 +123,7 @@ def tile_attend_at_quest_topk_kernel(tc, qT, k_words, k_scales, c_words, c_scale
         hi_scales.append(held.tile([P, HALF], U8, name="hi_scales1", align_bytes=64))
         quantise(hi_codes[1][:], hi_scales[1][:], hi_bf[1])
 
-        th_ps = psum.tile([P, P], F32, name="th_ps", offset=7 * BANK)
+        th_ps = psum.tile([P, P], F32, name="th_ps", offset=TH_BANK * BANK)
         nc.tensor.transpose(th_ps[:], th_rows[:], ident[:])
         neg_th = placed.tile([P, QB], F32, name="neg_th", offset=TH_HOME)
         nc.scalar.activation(out=neg_th[:], in_=th_ps[:, 0:QB], func=ACT.Copy, scale=-1.0)
@@ -142,31 +152,24 @@ def tile_attend_at_quest_topk_kernel(tc, qT, k_words, k_scales, c_words, c_scale
         y_bf = [placed.tile([P, HALF, PACK], BF16, name=f"y_bf{h}", offset=Y_HOME[h], align_bytes=64) for h in range(2)]
         y_codes, y_scales, v_gathered, v_pairs = [], [], [], []
 
-        def gate(c):
-            sig = held.tile([P, PACK, P], F32, name=f"sig{c}")
-            nc.scalar.activation(out=sig[:], in_=scores[c][:].rearrange("q (s t) -> q t s", t=PACK),
-                                 func=ACT.Sigmoid, bias=neg_th[:, c:c + 1])
-            return sig
-
-        def scale_on_vector(c):
-            sig = gate(c)
-            turned = psum.tile([P, PACK, P], F32, name=f"y_ps{c}", offset=(4 + c) * BANK)
-            for t in range(PACK):
-                nc.tensor.transpose(turned[:, t, :], sig[:, t, :], ident[:])
-            nc.vector.tensor_tensor(out=y_bf[0][:, c * P:(c + 1) * P, :], in0=turned[:].rearrange("p t q -> p q t"),
-                                    in1=us_col[:].unsqueeze(1).to_broadcast([P, P, PACK]), op=ALU.mult)
-
-        def scale_on_scalar():
-            turned = [psum.tile([P, 2, HALF], F32, name=f"y_ps{2 + u}", offset=(6 + u) * BANK) for u in range(2)]
+        def turn_gates(h):
+            turned = [psum.tile([P, 2, HALF], F32, name=f"y_ps{h}{u}", offset=(GATE_BANK + 2 * h + u) * BANK)
+                      for u in range(2)]
             for i in range(2):
-                sig = gate(2 + i)
+                c = 2 * h + i
+                sig = held.tile([P, PACK, P], F32, name=f"sig{c}")
+                nc.scalar.activation(out=sig[:], in_=scores[c][:].rearrange("q (s t) -> q t s", t=PACK),
+                                     func=ACT.Sigmoid, bias=neg_th[:, c:c + 1])
                 for t in range(PACK):
                     nc.tensor.transpose(turned[t // 2][:, t % 2, i * P:(i + 1) * P], sig[:, t, :], ident[:])
-            planes = held.tile([P, PACK, HALF], BF16, name="y_planes")
+            return turned
+
+        def scale_gates(h, turned):
+            y_rows = held.tile([P, PACK, HALF], BF16, name=f"y_rows{h}")
             for t in range(PACK):
-                nc.scalar.activation(out=planes[:, t, :], in_=turned[t // 2][:, t % 2, :], func=ACT.Copy,
+                nc.scalar.activation(out=y_rows[:, t, :], in_=turned[t // 2][:, t % 2, :], func=ACT.Copy,
                                      scale=us_col[:, t:t + 1])
-            return planes
+            return y_rows
 
         def quantise_gates(h):
             y_codes.append(held.tile([P, HALF], U32, name=f"y_codes{h}", align_bytes=64))
@@ -180,7 +183,7 @@ def tile_attend_at_quest_topk_kernel(tc, qT, k_words, k_scales, c_words, c_scale
 
         def turn_values(a):
             pairs = v_gathered[a][:].bitcast(F32)
-            v_ps = psum.tile([P, 2, P], F32, name=f"v_ps{a}", offset=(0, 6, 7, 3)[a] * BANK)
+            v_ps = psum.tile([P, 2, P], F32, name=f"v_ps{a}", offset=V_TURN_BANK[a] * BANK)
             for u in range(2):
                 nc.tensor.transpose(v_ps[:, u, :], pairs[:, u:SLOTS // 2:2], ident[:])
             v_b = held.tile([P, P, 2], F32, name=f"v_b{a}", align_bytes=64)
@@ -188,9 +191,9 @@ def tile_attend_at_quest_topk_kernel(tc, qT, k_words, k_scales, c_words, c_scale
             v_pairs.append(v_b)
 
         def quantise_values(a):
-            home = V_HOME[min(a + 1, EB - 1)] + (a % 2) * KB
+            home = V_HOME[2 + a // 2] + (a % 2) * KB
             v_codes = placed.tile([P, P], U32, name=f"v_codes{a}", offset=home, align_bytes=64)
-            v_scales = placed.tile([P, P], U8, name=f"v_scales{a}", offset=home + 512, align_bytes=64)
+            v_scales = placed.tile([P, P], U8, name=f"v_scales{a}", offset=home + 4 * P, align_bytes=64)
             quantise(v_codes[:], v_scales[:], v_pairs[a][:].rearrange("p e u -> p (e u)").bitcast(BF16))
             return v_codes, v_scales
 
@@ -209,23 +212,23 @@ def tile_attend_at_quest_topk_kernel(tc, qT, k_words, k_scales, c_words, c_scale
 
         gather_values(0)
         gather_values(1)
-        scale_on_vector(0)
-        scale_on_vector(1)
-        y_planes = scale_on_scalar()
-        quantise_gates(0)
+        y_turned = [turn_gates(h) for h in range(2)]
+        y_scaled = [scale_gates(h, y_turned[h]) for h in range(2)]
         gather_values(2)
-        nc.vector.tensor_copy(out=y_bf[1][:], in_=y_planes[:].rearrange("p t q -> p q t"))
-        turn_values(0)
-        turn_values(1)
-        turn_values(2)
-        first = quantise_values(0)
-        quantise_gates(1)
-        second = quantise_values(1)
-        multiply(0, first, [0, 1, 2, 3], 4, nc.scalar.copy, nc.sync)
-        multiply(1, second, [0, 1, 2, 3], 5, nc.scalar.copy, nc.sync)
+        for h in range(2):
+            nc.vector.tensor_copy(out=y_bf[h][:].rearrange("p (g i) t -> p g t i", i=RUN),
+                                  in_=y_scaled[h][:].rearrange("p t (g i) -> p g t i", i=RUN))
+        for a in range(EB - 1):
+            turn_values(a)
+        for h in range(2):
+            quantise_gates(h)
+        every_block = list(range(QB))
+        early = [quantise_values(a) for a in range(2)]
+        for a in range(2):
+            multiply(a, early[a], every_block, OUT_BANK[a], nc.scalar.copy, nc.sync)
         gather_values(3)
         turn_values(3)
-        multiply(2, quantise_values(2), [0, 1, 2, 3], 1, nc.scalar.copy, nc.sync)
+        multiply(2, quantise_values(2), every_block, OUT_BANK[2], nc.scalar.copy, nc.sync)
         last = quantise_values(3)
-        multiply(3, last, [0, 1], 2, nc.scalar.copy, nc.scalar)
-        multiply(3, last, [2, 3], 0, nc.vector.tensor_copy, nc.sync)
+        multiply(3, last, every_block[:2], LAST_OUT_BANK[0], nc.scalar.copy, nc.scalar)
+        multiply(3, last, every_block[2:], LAST_OUT_BANK[1], nc.vector.tensor_copy, nc.sync)

@@ -23,20 +23,16 @@ SCALE_ROWS, QUADRANT = 16, 32
 C_PLANE = 4
 
 KB = 1024
-Q_HOME, CS_HOME, KS_HOME, HI_HOME, TH_HOME = 0, 8 * KB, 12 * KB, 18 * KB, 22 * KB
-CW_HOME, KW_HOME = 23 * KB, 31 * KB
-V_HOME = (39 * KB, 63 * KB, 47 * KB, 55 * KB)
-US_HOME = 71 * KB
-LATE_END = US_HOME + 32
-Y_HOME = (V_HOME[2] + 2 * KB, V_HOME[2] + 4 * KB)
-VG_HOME = (HI_HOME + 2 * KB, V_HOME[0], TH_HOME, Y_HOME[1])
+Q_HOME, CW_HOME, KW_HOME = 0, 8 * KB, 16 * KB
+V_HOME = 24 * KB
+LATE_END = 56 * KB
+KS_HOME = LATE_END
 
 BANK = 2048
-GATE_BANK = QB
 TH_BANK = 7
-V_TURN_BANK = (0, 6, 7, 3)
-OUT_BANK = (4, 5, 1)
-LAST_OUT_BANK = (2, 0)
+V_TURN_BANK = (4, 5, 6, 7)
+OUT_BANK = (0, 1, 2)
+LAST_OUT_BANK = (3, 4)
 
 FLOPS = 2 * SLOTS * NQ * (2 * D + DV)
 
@@ -53,11 +49,13 @@ def tile_attend_at_quest_topk_kernel(tc, qT, k_words, k_scales, c_words, c_scale
 
         offsets = held.tile([P, SLOTS // 16], U16, name="offsets")
         nc.sync.dma_start(offsets[:], offs)
+        us_col = held.tile([P, PACK], F32, name="us_col")
+        nc.sync.dma_start(out=us_col[:], in_=us[0].rearrange("(p t) o -> p (t o)", t=PACK))
 
         ident = held.tile([P, P], F32, name="ident")
         th_rows = held.tile([P, P], F32, name="th_rows")
         warm = held.tile([P, 1], F32, name="warm")
-        cs_all = placed.tile([P, PAGES], U8, name="cs_all", offset=CS_HOME)
+        cs_all = held.tile([P, PAGES], U8, name="cs_all")
         ks_all = placed.tile([P, PAGES], U8, name="ks_all", offset=KS_HOME)
         zeros_a = placed.tile([P, P], F32, name="zeros_a", offset=Q_HOME)
         zeros_b = placed.tile([P, (LATE_END - CW_HOME) // 4], F32, name="zeros_b", offset=CW_HOME)
@@ -79,156 +77,156 @@ def tile_attend_at_quest_topk_kernel(tc, qT, k_words, k_scales, c_words, c_scale
         nc.sync.dma_start(out=q_raw[:], in_=qT[0].rearrange("(p j) q -> p j q", j=PACK))
         nc.sync.dma_start(out=th_rows[0:QB, :], in_=th[0, 0].rearrange("(c p) -> c p", p=P))
         for r in range(4):
-            nc.sync.dma_start(out=ks_all[r:P:QUADRANT, :].bitcast(I32),
-                              in_=k_scales[0, r:SCALE_ROWS:4, :].bitcast(I32))
+            nc.scalar.dma_start(out=ks_all[r:P:QUADRANT, :].bitcast(I32),
+                                in_=k_scales[0, r:SCALE_ROWS:4, :].bitcast(I32))
         cw_all = placed.tile([P, PAGES], I32, name="cw_all", offset=CW_HOME)
         nc.sync.dma_start(out=cw_all[:], in_=c_words[0].rearrange("p n t -> p (n t)").bitcast(I32))
         kw_all = placed.tile([P, PAGES], I32, name="kw_all", offset=KW_HOME)
         nc.sync.dma_start(out=kw_all[:], in_=k_words[0].rearrange("p n t -> p (n t)").bitcast(I32))
-        us_col = placed.tile([P, PACK], F32, name="us_col", offset=US_HOME)
-        nc.sync.dma_start(out=us_col[:], in_=us[0].rearrange("(p t) o -> p (t o)", t=PACK))
         v_all = []
         for a in range(EB):
-            v_tile = placed.tile([P, PAGES], F32, name=f"v_all{a}", offset=V_HOME[a])
+            v_tile = placed.tile([P, PAGES], F32, name=f"v_all{a}", offset=V_HOME + a * 8 * KB)
             nc.sync.dma_start(out=v_tile[:], in_=vT[a * P:(a + 1) * P, :])
             v_all.append(v_tile)
 
         cs_g = held.tile([P, SLOTS], U8, name="cs_g", align_bytes=64)
         nc.vector.tensor_copy(out=cs_g[:], in_=cs_all[:].indirect(offsets[:]))
 
-        lo_bf = placed.tile([P, NQ, PACK], BF16, name="lo_bf", offset=CS_HOME, align_bytes=64)
-        hi_bf = []
+        ks_g = held.tile([P, SLOTS], U8, name="ks_g", align_bytes=64)
+        nc.vector.tensor_copy(out=ks_g[:], in_=ks_all[:].indirect(offsets[:]))
+        lo_bf = placed.tile([P, NQ, PACK], BF16, name="lo_bf", offset=KS_HOME, align_bytes=64)
+        hi_bf = held.tile([P, NQ, PACK], BF16, name="hi_bf", align_bytes=64)
         for h in range(2):
             cols = slice(h * HALF, (h + 1) * HALF)
             source = q_raw[:, :, cols].rearrange("p j (g i) -> p g j i", i=RUN)
-            positive = placed.tile([P, HALF, PACK], BF16, name=f"hi_bf{h}", offset=HI_HOME + h * 2 * KB, align_bytes=64)
-            nc.scalar.activation(out=positive[:].rearrange("p (g i) j -> p g j i", i=RUN), in_=source, func=ACT.Relu)
+            nc.scalar.activation(out=hi_bf[:, cols, :].rearrange("p (g i) j -> p g j i", i=RUN), in_=source,
+                                 func=ACT.Relu)
             nc.vector.tensor_scalar_min(out=lo_bf[:, cols, :].rearrange("p (g i) j -> p g j i", i=RUN), in0=source,
                                         scalar1=0.0)
-            hi_bf.append(positive[:].rearrange("p q j -> p (q j)"))
-
-        ks_g = held.tile([P, SLOTS], U8, name="ks_g", align_bytes=64)
-        nc.vector.tensor_copy(out=ks_g[:], in_=ks_all[:].indirect(offsets[:]))
         lo_codes = held.tile([P, NQ], U32, name="lo_codes", align_bytes=64)
         lo_scales = held.tile([P, NQ], U8, name="lo_scales", align_bytes=64)
-        quantise(lo_codes[:], lo_scales[:], lo_bf[:].rearrange("p q j -> p (q j)"))
-        cw_g = placed.tile([P, SLOTS], U32, name="cw_g", offset=CS_HOME, align_bytes=64)
+        for h in range(2):
+            cols = slice(h * HALF, (h + 1) * HALF)
+            quantise(lo_codes[:, cols], lo_scales[:, cols], lo_bf[:, cols, :].rearrange("p q j -> p (q j)"))
+        hi_codes = [held.tile([P, HALF], U32, name="hi_codes0", align_bytes=64),
+                    placed.tile([P, HALF], U32, name="hi_codes1", offset=CW_HOME, align_bytes=64)]
+        hi_scales = [held.tile([P, HALF], U8, name=f"hi_scales{h}", align_bytes=64) for h in range(2)]
+        quantise(hi_codes[0][:], hi_scales[0][:], hi_bf[:, 0:HALF, :].rearrange("p q j -> p (q j)"))
+        cw_g = held.tile([P, SLOTS], U32, name="cw_g", align_bytes=64)
         nc.vector.tensor_copy(out=cw_g[:], in_=cw_all[:].bitcast(U32).indirect(offsets[:]))
-        hi_codes = [placed.tile([P, HALF], U32, name="hi_codes0", offset=KS_HOME, align_bytes=64)]
-        hi_scales = [placed.tile([P, HALF], U8, name="hi_scales0", offset=CW_HOME, align_bytes=64)]
-        quantise(hi_codes[0][:], hi_scales[0][:], hi_bf[0])
-        kw_g = placed.tile([P, SLOTS], U32, name="kw_g", offset=HI_HOME, align_bytes=64)
+        quantise(hi_codes[1][:], hi_scales[1][:], hi_bf[:, HALF:NQ, :].rearrange("p q j -> p (q j)"))
+        kw_g = held.tile([P, SLOTS], U32, name="kw_g", align_bytes=64)
         nc.vector.tensor_copy(out=kw_g[:], in_=kw_all[:].bitcast(U32).indirect(offsets[:]))
-        hi_codes.append(placed.tile([P, HALF], U32, name="hi_codes1", offset=KW_HOME, align_bytes=64))
-        hi_scales.append(held.tile([P, HALF], U8, name="hi_scales1", align_bytes=64))
-        quantise(hi_codes[1][:], hi_scales[1][:], hi_bf[1])
 
         th_ps = psum.tile([P, P], F32, name="th_ps", offset=TH_BANK * BANK)
         nc.tensor.transpose(th_ps[:], th_rows[:], ident[:])
-        neg_th = placed.tile([P, QB], F32, name="neg_th", offset=TH_HOME)
+        neg_th = held.tile([P, QB], F32, name="neg_th")
         nc.scalar.activation(out=neg_th[:], in_=th_ps[:, 0:QB], func=ACT.Copy, scale=-1.0)
+        us_laid = held.tile([P, P, PACK], F32, name="us_laid")
+        nc.scalar.copy(out=us_laid[:], in_=us_col[:].unsqueeze(1).to_broadcast([P, P, PACK]))
 
         scores = [psum.tile([P, SLOTS], F32, name=f"score{c}", offset=c * BANK) for c in range(QB)]
-
-        def score_low(c):
+        for c in range(QB):
             cols = slice(c * P, (c + 1) * P)
             nc.tensor.matmul_mx(out=scores[c][:], lhsT=lo_codes[:, cols].bitcast(FP8X4), lhsT_scale=lo_scales[:, cols],
                                 rhs=cw_g[:].bitcast(FP8X4), rhs_scale=cs_g[C_PLANE:P, :], start=True, stop=False)
-
-        def score_high(c):
+        for c in range(QB):
             cols = slice(c % 2 * P, (c % 2 + 1) * P)
             nc.tensor.matmul_mx(out=scores[c][:], lhsT=hi_codes[c // 2][:, cols].bitcast(FP8X4),
                                 lhsT_scale=hi_scales[c // 2][:, cols],
                                 rhs=kw_g[:].bitcast(FP8X4), rhs_scale=ks_g[:], start=False, stop=True)
 
-        for c in range(QB - 1):
-            score_low(c)
-        for c in range(QB - 1):
-            score_high(c)
-        score_low(QB - 1)
-        score_high(QB - 1)
-
         out_rows = out[0].rearrange("(c p) e -> p c e", p=P)
-        y_bf = [placed.tile([P, HALF, PACK], BF16, name=f"y_bf{h}", offset=Y_HOME[h], align_bytes=64) for h in range(2)]
-        y_codes, y_scales, v_gathered, v_pairs = [], [], [], []
+        y_bf = [placed.tile([P, HALF, PACK], BF16, name=f"y_bf{h}", offset=V_HOME + h * 2 * KB, align_bytes=64)
+                for h in range(2)]
+        y_codes = [held.tile([P, HALF], U32, name=f"y_codes{h}", align_bytes=64) for h in range(2)]
+        y_scales = [held.tile([P, HALF], U8, name=f"y_scales{h}", align_bytes=64) for h in range(2)]
+        v_g = [held.tile([P, SLOTS], BF16, name=f"v_g{a}") for a in range(EB)]
 
-        def turn_gates(h):
-            turned = [psum.tile([P, 2, HALF], F32, name=f"y_ps{h}{u}", offset=(GATE_BANK + 2 * h + u) * BANK)
-                      for u in range(2)]
-            for i in range(2):
-                c = 2 * h + i
-                sig = held.tile([P, PACK, P], F32, name=f"sig{c}")
-                nc.scalar.activation(out=sig[:], in_=scores[c][:].rearrange("q (s t) -> q t s", t=PACK),
-                                     func=ACT.Sigmoid, bias=neg_th[:, c:c + 1])
-                for t in range(PACK):
-                    nc.tensor.transpose(turned[t // 2][:, t % 2, i * P:(i + 1) * P], sig[:, t, :], ident[:])
+        def gate(c):
+            sig = held.tile([P, PACK, P], F32, name=f"sig{c}")
+            nc.scalar.activation(out=sig[:], in_=scores[c][:].rearrange("q (s t) -> q t s", t=PACK),
+                                 func=ACT.Sigmoid, bias=neg_th[:, c:c + 1])
+            return sig
+
+        def turn_gate(c, sig):
+            turned = psum.tile([P, PACK, P], F32, name=f"y_ps{c}", offset=c * BANK)
+            for t in range(PACK):
+                nc.tensor.transpose(turned[:, t, :], sig[:, t, :], ident[:])
             return turned
 
-        def scale_gates(h, turned):
-            y_rows = held.tile([P, PACK, HALF], BF16, name=f"y_rows{h}")
-            for t in range(PACK):
-                nc.scalar.activation(out=y_rows[:, t, :], in_=turned[t // 2][:, t % 2, :], func=ACT.Copy,
-                                     scale=us_col[:, t:t + 1])
-            return y_rows
+        def scale_gate(c, turned):
+            nc.vector.tensor_tensor(out=y_bf[c // 2][:, c % 2 * P:(c % 2 + 1) * P, :],
+                                    in0=turned[:].rearrange("p t q -> p q t"), in1=us_laid[:], op=ALU.mult)
 
         def quantise_gates(h):
-            y_codes.append(held.tile([P, HALF], U32, name=f"y_codes{h}", align_bytes=64))
-            y_scales.append(held.tile([P, HALF], U8, name=f"y_scales{h}", align_bytes=64))
             quantise(y_codes[h][:], y_scales[h][:], y_bf[h][:].rearrange("p q t -> p (q t)"))
 
-        def gather_values(a):
-            v_g = placed.tile([P, SLOTS], BF16, name=f"v_g{a}", offset=VG_HOME[a])
-            nc.vector.tensor_copy(out=v_g[:], in_=v_all[a][:].indirect(offsets[:]))
-            v_gathered.append(v_g)
+        def gather_on_vector(a, first, last):
+            nc.vector.tensor_copy(out=v_g[a][:, first:last], in_=v_all[a][:].indirect(offsets[:, first // 16:last // 16]))
+
+        def gather_on_scalar(a, first, last):
+            nc.scalar.activation(out=v_g[a][:, first:last], in_=v_all[a][:].indirect(offsets[:, first // 16:last // 16]),
+                                 func=ACT.Copy)
 
         def turn_values(a):
-            pairs = v_gathered[a][:].bitcast(F32)
+            pairs = v_g[a][:].bitcast(F32)
             v_ps = psum.tile([P, 2, P], F32, name=f"v_ps{a}", offset=V_TURN_BANK[a] * BANK)
             for u in range(2):
                 nc.tensor.transpose(v_ps[:, u, :], pairs[:, u:SLOTS // 2:2], ident[:])
-            v_b = held.tile([P, P, 2], F32, name=f"v_b{a}", align_bytes=64)
-            nc.scalar.copy(out=v_b[:], in_=v_ps[:].rearrange("p u e -> p e u"))
-            v_pairs.append(v_b)
+            return v_ps
 
-        def quantise_values(a):
-            home = V_HOME[2 + a // 2] + (a % 2) * KB
-            v_codes = placed.tile([P, P], U32, name=f"v_codes{a}", offset=home, align_bytes=64)
-            v_scales = placed.tile([P, P], U8, name=f"v_scales{a}", offset=home + 4 * P, align_bytes=64)
-            quantise(v_codes[:], v_scales[:], v_pairs[a][:].rearrange("p e u -> p (e u)").bitcast(BF16))
+        def lay_values(words, v_ps):
+            nc.scalar.copy(out=words, in_=v_ps[:].rearrange("p u e -> p e u"))
+
+        def quantise_values(name, words):
+            width = words.shape[1]
+            v_codes = held.tile([P, width], U32, name="v_codes" + name, align_bytes=64)
+            v_scales = held.tile([P, width], U8, name="v_scales" + name, align_bytes=64)
+            quantise(v_codes[:], v_scales[:], words.rearrange("p e u -> p (e u)").bitcast(BF16))
             return v_codes, v_scales
 
-        def multiply(a, operand, blocks, bank, copy, queue):
+        def multiply(first, operand, blocks, bank, copy, queue, home):
             v_codes, v_scales = operand
-            name = f"{a}_{blocks[0]}"
-            acc = psum.tile([P, len(blocks), P], F32, name="out_ps" + name, offset=bank * BANK)
+            width = v_codes.shape[1]
+            name = f"{first}_{blocks[0]}"
+            acc = psum.tile([P, len(blocks), width], F32, name="out_ps" + name, offset=bank * BANK)
             for i, c in enumerate(blocks):
                 cols = slice(c % 2 * P, (c % 2 + 1) * P)
                 nc.tensor.matmul_mx(out=acc[:, i, :], lhsT=y_codes[c // 2][:, cols].bitcast(FP8X4),
                                     lhsT_scale=y_scales[c // 2][:, cols],
                                     rhs=v_codes[:].bitcast(FP8X4), rhs_scale=v_scales[:], start=True, stop=True)
-            result = held.tile([P, len(blocks), P], F32, name="result" + name)
+            result = placed.tile([P, len(blocks), width], F32, name="result" + name, offset=home)
             copy(out=result[:], in_=acc[:])
-            queue.dma_start(out=out_rows[:, blocks[0]:blocks[-1] + 1, a * P:(a + 1) * P], in_=result[:])
+            queue.dma_start(out=out_rows[:, blocks[0]:blocks[-1] + 1, first:first + width], in_=result[:])
 
-        gather_values(0)
-        gather_values(1)
-        y_turned = [turn_gates(h) for h in range(2)]
-        y_scaled = [scale_gates(h, y_turned[h]) for h in range(2)]
-        gather_values(2)
-        for h in range(2):
-            nc.vector.tensor_copy(out=y_bf[h][:].rearrange("p (g i) t -> p g t i", i=RUN),
-                                  in_=y_scaled[h][:].rearrange("p t (g i) -> p g t i", i=RUN))
-        for a in range(EB - 1):
-            turn_values(a)
-        for h in range(2):
-            quantise_gates(h)
         every_block = list(range(QB))
-        early = [quantise_values(a) for a in range(2)]
+        sigs = [gate(c) for c in range(QB)]
+        gather_on_vector(0, 0, SLOTS)
+        turned = [turn_gate(c, sigs[c]) for c in range(QB)]
+        for c in range(QB - 1):
+            scale_gate(c, turned[c])
+        quantise_gates(0)
+        scale_gate(QB - 1, turned[QB - 1])
+        quantise_gates(1)
+        gather_on_scalar(1, 0, SLOTS)
+        v_early = placed.tile([P, 2 * P, 2], F32, name="v_early", offset=V_HOME + 8 * KB, align_bytes=64)
         for a in range(2):
-            multiply(a, early[a], every_block, OUT_BANK[a], nc.scalar.copy, nc.sync)
-        gather_values(3)
-        turn_values(3)
-        multiply(2, quantise_values(2), every_block, OUT_BANK[2], nc.scalar.copy, nc.sync)
-        last = quantise_values(3)
-        multiply(3, last, every_block[:2], LAST_OUT_BANK[0], nc.scalar.copy, nc.scalar)
-        multiply(3, last, every_block[2:], LAST_OUT_BANK[1], nc.vector.tensor_copy, nc.sync)
+            lay_values(v_early[:, a * P:(a + 1) * P, :], turn_values(a))
+        early = quantise_values("early", v_early[:])
+        gather_on_vector(2, 0, SLOTS)
+        multiply(0, early, every_block[:2], OUT_BANK[0], nc.scalar.copy, nc.sync, Q_HOME)
+        v_ps2 = turn_values(2)
+        gather_on_vector(3, 0, SLOTS // 2)
+        gather_on_scalar(3, SLOTS // 2, SLOTS)
+        v_ps3 = turn_values(3)
+        multiply(0, early, every_block[2:], OUT_BANK[1], nc.vector.tensor_copy, nc.sync, V_HOME + 28 * KB)
+        v_late = [placed.tile([P, P, 2], F32, name=f"v_late{a}", offset=V_HOME + (24 + a) * KB, align_bytes=64)
+                  for a in range(2)]
+        lay_values(v_late[0][:], v_ps2)
+        lay_values(v_late[1][:], v_ps3)
+        operand2 = quantise_values("2", v_late[0][:])
+        last = quantise_values("3", v_late[1][:])
+        multiply(2 * P, operand2, every_block, OUT_BANK[2], nc.scalar.copy, nc.sync, Q_HOME + 2 * KB)
+        multiply(3 * P, last, every_block[:2], LAST_OUT_BANK[0], nc.scalar.copy, nc.scalar, Q_HOME + 4 * KB)
+        multiply(3 * P, last, every_block[2:], LAST_OUT_BANK[1], nc.vector.tensor_copy, nc.sync, Q_HOME + 6 * KB)

@@ -25,8 +25,8 @@ C_PLANE = 4
 KB = 1024
 Q_HOME, CW_HOME, KW_HOME = 0, 8 * KB, 16 * KB
 V_HOME = 24 * KB
-LATE_END = 56 * KB
-KS_HOME = LATE_END
+US_HOME = 56 * KB
+LATE_END = US_HOME + 32
 
 BANK = 2048
 TH_BANK = 7
@@ -49,15 +49,13 @@ def tile_attend_at_quest_topk_kernel(tc, qT, k_words, k_scales, c_words, c_scale
 
         offsets = held.tile([P, SLOTS // 16], U16, name="offsets")
         nc.sync.dma_start(offsets[:], offs)
-        us_col = held.tile([P, PACK], F32, name="us_col")
-        nc.sync.dma_start(out=us_col[:], in_=us[0].rearrange("(p t) o -> p (t o)", t=PACK))
 
         ident = held.tile([P, P], F32, name="ident")
         th_rows = held.tile([P, P], F32, name="th_rows")
         warm = held.tile([P, 1], F32, name="warm")
         cs_all = held.tile([P, PAGES], U8, name="cs_all")
-        ks_all = placed.tile([P, PAGES], U8, name="ks_all", offset=KS_HOME)
-        zeros_a = placed.tile([P, P], F32, name="zeros_a", offset=Q_HOME)
+        ks_all = held.tile([P, PAGES], U8, name="ks_all")
+        zeros_a = placed.tile([P, P], F32, name="zeros_a", offset=Q_HOME + 4 * KB - 256)
         zeros_b = placed.tile([P, (LATE_END - CW_HOME) // 4], F32, name="zeros_b", offset=CW_HOME)
         nc.vector.memset(warm[:], 0.0)
         nc.scalar.activation(out=warm[:], in_=warm[:], func=ACT.Sigmoid)
@@ -73,16 +71,22 @@ def tile_attend_at_quest_topk_kernel(tc, qT, k_words, k_scales, c_words, c_scale
             queue = nc.sync if r < 2 else nc.scalar
             queue.dma_start(out=cs_all[C_PLANE + r:P:QUADRANT, :].bitcast(I32),
                             in_=c_scales[0, r:SCALE_ROWS:4, :].bitcast(I32))
-        q_raw = placed.tile([P, PACK, NQ], F32, name="q_raw", offset=Q_HOME)
-        nc.sync.dma_start(out=q_raw[:], in_=qT[0].rearrange("(p j) q -> p j q", j=PACK))
+        q_rows = qT[0].rearrange("(p j) q -> p j q", j=PACK)
+        q_raw = []
+        for u in range(2):
+            q_pair = placed.tile([P, 2, NQ], F32, name=f"q_raw{u}", offset=Q_HOME + u * 4 * KB)
+            nc.sync.dma_start(out=q_pair[:], in_=q_rows[:, 2 * u:2 * u + 2, :])
+            q_raw.append(q_pair)
         nc.sync.dma_start(out=th_rows[0:QB, :], in_=th[0, 0].rearrange("(c p) -> c p", p=P))
         for r in range(4):
-            nc.scalar.dma_start(out=ks_all[r:P:QUADRANT, :].bitcast(I32),
-                                in_=k_scales[0, r:SCALE_ROWS:4, :].bitcast(I32))
+            nc.sync.dma_start(out=ks_all[r:P:QUADRANT, :].bitcast(I32),
+                              in_=k_scales[0, r:SCALE_ROWS:4, :].bitcast(I32))
         cw_all = placed.tile([P, PAGES], I32, name="cw_all", offset=CW_HOME)
         nc.sync.dma_start(out=cw_all[:], in_=c_words[0].rearrange("p n t -> p (n t)").bitcast(I32))
         kw_all = placed.tile([P, PAGES], I32, name="kw_all", offset=KW_HOME)
         nc.sync.dma_start(out=kw_all[:], in_=k_words[0].rearrange("p n t -> p (n t)").bitcast(I32))
+        us_col = placed.tile([P, PACK], F32, name="us_col", offset=US_HOME)
+        nc.sync.dma_start(out=us_col[:], in_=us[0].rearrange("(p t) o -> p (t o)", t=PACK))
         v_all = []
         for a in range(EB):
             v_tile = placed.tile([P, PAGES], F32, name=f"v_all{a}", offset=V_HOME + a * 8 * KB)
@@ -92,29 +96,22 @@ def tile_attend_at_quest_topk_kernel(tc, qT, k_words, k_scales, c_words, c_scale
         cs_g = held.tile([P, SLOTS], U8, name="cs_g", align_bytes=64)
         nc.vector.tensor_copy(out=cs_g[:], in_=cs_all[:].indirect(offsets[:]))
 
+        lo_bf = held.tile([P, NQ, PACK], BF16, name="lo_bf", align_bytes=64)
+        hi_bf = held.tile([P, NQ, PACK], BF16, name="hi_bf", align_bytes=64)
+        for u in range(2):
+            source = q_raw[u][:].rearrange("p e q -> p q e")
+            nc.scalar.activation(out=hi_bf[:, :, 2 * u:2 * u + 2], in_=source, func=ACT.Relu)
+            nc.vector.tensor_scalar_min(out=lo_bf[:, :, 2 * u:2 * u + 2], in0=source, scalar1=0.0)
         ks_g = held.tile([P, SLOTS], U8, name="ks_g", align_bytes=64)
         nc.vector.tensor_copy(out=ks_g[:], in_=ks_all[:].indirect(offsets[:]))
-        lo_bf = placed.tile([P, NQ, PACK], BF16, name="lo_bf", offset=KS_HOME, align_bytes=64)
-        hi_bf = held.tile([P, NQ, PACK], BF16, name="hi_bf", align_bytes=64)
-        for h in range(2):
-            cols = slice(h * HALF, (h + 1) * HALF)
-            source = q_raw[:, :, cols].rearrange("p j (g i) -> p g j i", i=RUN)
-            nc.scalar.activation(out=hi_bf[:, cols, :].rearrange("p (g i) j -> p g j i", i=RUN), in_=source,
-                                 func=ACT.Relu)
-            nc.vector.tensor_scalar_min(out=lo_bf[:, cols, :].rearrange("p (g i) j -> p g j i", i=RUN), in0=source,
-                                        scalar1=0.0)
         lo_codes = held.tile([P, NQ], U32, name="lo_codes", align_bytes=64)
         lo_scales = held.tile([P, NQ], U8, name="lo_scales", align_bytes=64)
-        for h in range(2):
-            cols = slice(h * HALF, (h + 1) * HALF)
-            quantise(lo_codes[:, cols], lo_scales[:, cols], lo_bf[:, cols, :].rearrange("p q j -> p (q j)"))
-        hi_codes = [held.tile([P, HALF], U32, name="hi_codes0", align_bytes=64),
-                    placed.tile([P, HALF], U32, name="hi_codes1", offset=CW_HOME, align_bytes=64)]
-        hi_scales = [held.tile([P, HALF], U8, name=f"hi_scales{h}", align_bytes=64) for h in range(2)]
-        quantise(hi_codes[0][:], hi_scales[0][:], hi_bf[:, 0:HALF, :].rearrange("p q j -> p (q j)"))
+        quantise(lo_codes[:], lo_scales[:], lo_bf[:].rearrange("p q j -> p (q j)"))
         cw_g = held.tile([P, SLOTS], U32, name="cw_g", align_bytes=64)
         nc.vector.tensor_copy(out=cw_g[:], in_=cw_all[:].bitcast(U32).indirect(offsets[:]))
-        quantise(hi_codes[1][:], hi_scales[1][:], hi_bf[:, HALF:NQ, :].rearrange("p q j -> p (q j)"))
+        hi_codes = placed.tile([P, NQ], U32, name="hi_codes", offset=CW_HOME, align_bytes=64)
+        hi_scales = held.tile([P, NQ], U8, name="hi_scales", align_bytes=64)
+        quantise(hi_codes[:], hi_scales[:], hi_bf[:].rearrange("p q j -> p (q j)"))
         kw_g = held.tile([P, SLOTS], U32, name="kw_g", align_bytes=64)
         nc.vector.tensor_copy(out=kw_g[:], in_=kw_all[:].bitcast(U32).indirect(offsets[:]))
 
@@ -131,9 +128,8 @@ def tile_attend_at_quest_topk_kernel(tc, qT, k_words, k_scales, c_words, c_scale
             nc.tensor.matmul_mx(out=scores[c][:], lhsT=lo_codes[:, cols].bitcast(FP8X4), lhsT_scale=lo_scales[:, cols],
                                 rhs=cw_g[:].bitcast(FP8X4), rhs_scale=cs_g[C_PLANE:P, :], start=True, stop=False)
         for c in range(QB):
-            cols = slice(c % 2 * P, (c % 2 + 1) * P)
-            nc.tensor.matmul_mx(out=scores[c][:], lhsT=hi_codes[c // 2][:, cols].bitcast(FP8X4),
-                                lhsT_scale=hi_scales[c // 2][:, cols],
+            cols = slice(c * P, (c + 1) * P)
+            nc.tensor.matmul_mx(out=scores[c][:], lhsT=hi_codes[:, cols].bitcast(FP8X4), lhsT_scale=hi_scales[:, cols],
                                 rhs=kw_g[:].bitcast(FP8X4), rhs_scale=ks_g[:], start=False, stop=True)
 
         out_rows = out[0].rearrange("(c p) e -> p c e", p=P)

@@ -28,11 +28,12 @@ V_HOME = 24 * KB
 US_HOME = 56 * KB
 LATE_END = US_HOME + 32
 
+LAST_SPLIT = 320
 BANK = 2048
 TH_BANK = 7
-V_TURN_BANK = (4, 5, 6, 7)
-OUT_BANK = (0, 1, 2)
-LAST_OUT_BANK = (3, 4)
+V_TURN_BANK = (1, 5, 6, 7)
+OUT_BANK = (0, 4, 2)
+LAST_OUT_BANK = (3, 1)
 
 FLOPS = 2 * SLOTS * NQ * (2 * D + DV)
 
@@ -50,19 +51,24 @@ def tile_attend_at_quest_topk_kernel(tc, qT, k_words, k_scales, c_words, c_scale
         offsets = held.tile([P, SLOTS // 16], U16, name="offsets")
         nc.sync.dma_start(offsets[:], offs)
 
+        q_rows = qT[0].rearrange("(p j) q -> p j q", j=PACK)
+        q_raw = [held.tile([P, 2, NQ], F32, name="q_raw0"),
+                 placed.tile([P, 2, NQ], F32, name="q_raw1", offset=Q_HOME)]
+        nc.sync.dma_start(out=q_raw[0][:], in_=q_rows[:, 0:2, :])
+
         ident = held.tile([P, P], F32, name="ident")
         th_rows = held.tile([P, P], F32, name="th_rows")
         warm = held.tile([P, 1], F32, name="warm")
         cs_all = held.tile([P, PAGES], U8, name="cs_all")
         ks_all = held.tile([P, PAGES], U8, name="ks_all")
-        zeros_a = placed.tile([P, P], F32, name="zeros_a", offset=Q_HOME + 4 * KB - 256)
-        zeros_b = placed.tile([P, (LATE_END - CW_HOME) // 4], F32, name="zeros_b", offset=CW_HOME)
+        zeros_a = placed.tile([P, (KW_HOME - Q_HOME) // 4], F32, name="zeros_a", offset=Q_HOME)
+        zeros_b = placed.tile([P, (LATE_END - KW_HOME) // 4], F32, name="zeros_b", offset=KW_HOME)
         nc.vector.memset(warm[:], 0.0)
         nc.scalar.activation(out=warm[:], in_=warm[:], func=ACT.Sigmoid)
-        nc.gpsimd.memset(zeros_a[:], 0.0)
+        nc.gpsimd.memset(zeros_a[:, 0:P], 0.0)
+        nc.gpsimd.memset(cs_all[:].bitcast(I32), 0)
+        nc.gpsimd.tensor_copy(out=th_rows[:], in_=zeros_a[:, 0:P])
         nc.gpsimd.memset(zeros_b[:, 0:P], 0.0)
-        nc.vector.memset(cs_all[:].bitcast(I32), 0)
-        nc.vector.tensor_copy(out=th_rows[:], in_=zeros_a[:])
         nc.gpsimd.memset(ks_all[:].bitcast(I32), 0)
         nc.gpsimd.affine_select(out=ident[:], in_=zeros_b[:, 0:P], compare_op=ALU.not_equal, fill=1.0, base=0,
                                 pattern=[[-1, P]], channel_multiplier=1)
@@ -71,18 +77,13 @@ def tile_attend_at_quest_topk_kernel(tc, qT, k_words, k_scales, c_words, c_scale
             queue = nc.sync if r < 2 else nc.scalar
             queue.dma_start(out=cs_all[C_PLANE + r:P:QUADRANT, :].bitcast(I32),
                             in_=c_scales[0, r:SCALE_ROWS:4, :].bitcast(I32))
-        q_rows = qT[0].rearrange("(p j) q -> p j q", j=PACK)
-        q_raw = []
-        for u in range(2):
-            q_pair = placed.tile([P, 2, NQ], F32, name=f"q_raw{u}", offset=Q_HOME + u * 4 * KB)
-            nc.sync.dma_start(out=q_pair[:], in_=q_rows[:, 2 * u:2 * u + 2, :])
-            q_raw.append(q_pair)
+        nc.sync.dma_start(out=q_raw[1][:], in_=q_rows[:, 2:4, :])
         nc.sync.dma_start(out=th_rows[0:QB, :], in_=th[0, 0].rearrange("(c p) -> c p", p=P))
+        cw_all = placed.tile([P, PAGES], I32, name="cw_all", offset=CW_HOME)
+        nc.sync.dma_start(out=cw_all[:], in_=c_words[0].rearrange("p n t -> p (n t)").bitcast(I32))
         for r in range(4):
             nc.sync.dma_start(out=ks_all[r:P:QUADRANT, :].bitcast(I32),
                               in_=k_scales[0, r:SCALE_ROWS:4, :].bitcast(I32))
-        cw_all = placed.tile([P, PAGES], I32, name="cw_all", offset=CW_HOME)
-        nc.sync.dma_start(out=cw_all[:], in_=c_words[0].rearrange("p n t -> p (n t)").bitcast(I32))
         kw_all = placed.tile([P, PAGES], I32, name="kw_all", offset=KW_HOME)
         nc.sync.dma_start(out=kw_all[:], in_=k_words[0].rearrange("p n t -> p (n t)").bitcast(I32))
         us_col = placed.tile([P, PACK], F32, name="us_col", offset=US_HOME)
@@ -93,25 +94,28 @@ def tile_attend_at_quest_topk_kernel(tc, qT, k_words, k_scales, c_words, c_scale
             nc.sync.dma_start(out=v_tile[:], in_=vT[a * P:(a + 1) * P, :])
             v_all.append(v_tile)
 
-        cs_g = held.tile([P, SLOTS], U8, name="cs_g", align_bytes=64)
-        nc.vector.tensor_copy(out=cs_g[:], in_=cs_all[:].indirect(offsets[:]))
-
         lo_bf = held.tile([P, NQ, PACK], BF16, name="lo_bf", align_bytes=64)
         hi_bf = held.tile([P, NQ, PACK], BF16, name="hi_bf", align_bytes=64)
-        for u in range(2):
+
+        def split_queries(u):
             source = q_raw[u][:].rearrange("p e q -> p q e")
             nc.scalar.activation(out=hi_bf[:, :, 2 * u:2 * u + 2], in_=source, func=ACT.Relu)
             nc.vector.tensor_scalar_min(out=lo_bf[:, :, 2 * u:2 * u + 2], in0=source, scalar1=0.0)
-        ks_g = held.tile([P, SLOTS], U8, name="ks_g", align_bytes=64)
-        nc.vector.tensor_copy(out=ks_g[:], in_=ks_all[:].indirect(offsets[:]))
+
+        split_queries(0)
+        cs_g = held.tile([P, SLOTS], U8, name="cs_g", align_bytes=64)
+        nc.vector.tensor_copy(out=cs_g[:], in_=cs_all[:].indirect(offsets[:]))
+        split_queries(1)
         lo_codes = held.tile([P, NQ], U32, name="lo_codes", align_bytes=64)
         lo_scales = held.tile([P, NQ], U8, name="lo_scales", align_bytes=64)
         quantise(lo_codes[:], lo_scales[:], lo_bf[:].rearrange("p q j -> p (q j)"))
-        cw_g = held.tile([P, SLOTS], U32, name="cw_g", align_bytes=64)
-        nc.vector.tensor_copy(out=cw_g[:], in_=cw_all[:].bitcast(U32).indirect(offsets[:]))
-        hi_codes = placed.tile([P, NQ], U32, name="hi_codes", offset=CW_HOME, align_bytes=64)
+        hi_codes = held.tile([P, NQ], U32, name="hi_codes", align_bytes=64)
         hi_scales = held.tile([P, NQ], U8, name="hi_scales", align_bytes=64)
         quantise(hi_codes[:], hi_scales[:], hi_bf[:].rearrange("p q j -> p (q j)"))
+        cw_g = held.tile([P, SLOTS], U32, name="cw_g", align_bytes=64)
+        nc.vector.tensor_copy(out=cw_g[:], in_=cw_all[:].bitcast(U32).indirect(offsets[:]))
+        ks_g = held.tile([P, SLOTS], U8, name="ks_g", align_bytes=64)
+        nc.vector.tensor_copy(out=ks_g[:], in_=ks_all[:].indirect(offsets[:]))
         kw_g = held.tile([P, SLOTS], U32, name="kw_g", align_bytes=64)
         nc.vector.tensor_copy(out=kw_g[:], in_=kw_all[:].bitcast(U32).indirect(offsets[:]))
 
@@ -172,12 +176,12 @@ def tile_attend_at_quest_topk_kernel(tc, qT, k_words, k_scales, c_words, c_scale
                 nc.tensor.transpose(v_ps[:, u, :], pairs[:, u:SLOTS // 2:2], ident[:])
             return v_ps
 
-        def lay_values(words, v_ps):
-            nc.scalar.copy(out=words, in_=v_ps[:].rearrange("p u e -> p e u"))
+        def lay_values(words, v_ps, copy):
+            copy(out=words, in_=v_ps[:].rearrange("p u e -> p e u"))
 
-        def quantise_values(name, words):
+        def quantise_values(name, words, home):
             width = words.shape[1]
-            v_codes = held.tile([P, width], U32, name="v_codes" + name, align_bytes=64)
+            v_codes = placed.tile([P, width], U32, name="v_codes" + name, offset=home, align_bytes=64)
             v_scales = held.tile([P, width], U8, name="v_scales" + name, align_bytes=64)
             quantise(v_codes[:], v_scales[:], words.rearrange("p e u -> p (e u)").bitcast(BF16))
             return v_codes, v_scales
@@ -204,25 +208,27 @@ def tile_attend_at_quest_topk_kernel(tc, qT, k_words, k_scales, c_words, c_scale
             scale_gate(c, turned[c])
         quantise_gates(0)
         scale_gate(QB - 1, turned[QB - 1])
+        v_words = [held.tile([P, P, 2], F32, name=f"v_words{a}", align_bytes=64) for a in range(2)]
+        v_words.extend(placed.tile([P, P, 2], F32, name=f"v_words{a}", offset=V_HOME + (22 + 2 * (a - 1)) * KB, align_bytes=64)
+                       for a in range(2, EB))
+        lay_values(v_words[0][:], turn_values(0), nc.vector.tensor_copy)
         quantise_gates(1)
         gather_on_scalar(1, 0, SLOTS)
-        v_early = placed.tile([P, 2 * P, 2], F32, name="v_early", offset=V_HOME + 8 * KB, align_bytes=64)
-        for a in range(2):
-            lay_values(v_early[:, a * P:(a + 1) * P, :], turn_values(a))
-        early = quantise_values("early", v_early[:])
-        gather_on_vector(2, 0, SLOTS)
-        multiply(0, early, every_block[:2], OUT_BANK[0], nc.scalar.copy, nc.sync, Q_HOME)
+        v_ps1 = turn_values(1)
+        operand0 = quantise_values("0", v_words[0][:], V_HOME + 8 * KB)
+        lay_values(v_words[1][:], v_ps1, nc.vector.tensor_copy)
+        gather_on_scalar(2, 0, SLOTS)
         v_ps2 = turn_values(2)
-        gather_on_vector(3, 0, SLOTS // 2)
-        gather_on_scalar(3, SLOTS // 2, SLOTS)
+        operand1 = quantise_values("1", v_words[1][:], V_HOME + 16 * KB)
+        gather_on_vector(3, 0, LAST_SPLIT)
+        gather_on_scalar(3, LAST_SPLIT, SLOTS)
         v_ps3 = turn_values(3)
-        multiply(0, early, every_block[2:], OUT_BANK[1], nc.vector.tensor_copy, nc.sync, V_HOME + 28 * KB)
-        v_late = [placed.tile([P, P, 2], F32, name=f"v_late{a}", offset=V_HOME + (24 + a) * KB, align_bytes=64)
-                  for a in range(2)]
-        lay_values(v_late[0][:], v_ps2)
-        lay_values(v_late[1][:], v_ps3)
-        operand2 = quantise_values("2", v_late[0][:])
-        last = quantise_values("3", v_late[1][:])
+        lay_values(v_words[2][:], v_ps2, nc.vector.tensor_copy)
+        multiply(0, operand0, every_block, OUT_BANK[0], nc.scalar.copy, nc.sync, V_HOME + 28 * KB)
+        operand2 = quantise_values("2", v_words[2][:], Q_HOME + KB)
+        multiply(P, operand1, every_block, OUT_BANK[1], nc.vector.tensor_copy, nc.sync, V_HOME + 24 * KB)
+        lay_values(v_words[3][:], v_ps3, nc.scalar.copy)
+        last = quantise_values("3", v_words[3][:], Q_HOME + 3 * KB // 2)
         multiply(2 * P, operand2, every_block, OUT_BANK[2], nc.scalar.copy, nc.sync, Q_HOME + 2 * KB)
         multiply(3 * P, last, every_block[:2], LAST_OUT_BANK[0], nc.scalar.copy, nc.scalar, Q_HOME + 4 * KB)
         multiply(3 * P, last, every_block[2:], LAST_OUT_BANK[1], nc.vector.tensor_copy, nc.sync, Q_HOME + 6 * KB)

@@ -28,11 +28,12 @@ V_HOME = 24 * KB
 US_HOME = 56 * KB
 LATE_END = US_HOME + 32
 
-LAST_SPLIT = 320
+TH_HOME = 57 * KB
+LAST_SPLIT = 288
 BANK = 2048
 TH_BANK = 7
 V_TURN_BANK = (1, 5, 6, 7)
-OUT_BANK = (0, 4, 2)
+OUT_BANK = (0, 4, 2, 5)
 LAST_OUT_BANK = (3, 1)
 
 FLOPS = 2 * SLOTS * NQ * (2 * D + DV)
@@ -48,16 +49,15 @@ def tile_attend_at_quest_topk_kernel(tc, qT, k_words, k_scales, c_words, c_scale
         def quantise(codes, scales, values):
             nc.vector.quantize_mx(out=codes.bitcast(FP8X4), scales=scales, in_=values)
 
-        offsets = held.tile([P, SLOTS // 16], U16, name="offsets")
-        nc.sync.dma_start(offsets[:], offs)
-
         q_rows = qT[0].rearrange("(p j) q -> p j q", j=PACK)
         q_raw = [held.tile([P, 2, NQ], F32, name="q_raw0"),
                  placed.tile([P, 2, NQ], F32, name="q_raw1", offset=Q_HOME)]
         nc.sync.dma_start(out=q_raw[0][:], in_=q_rows[:, 0:2, :])
+        offsets = held.tile([P, SLOTS // 16], U16, name="offsets")
+        nc.sync.dma_start(offsets[:], offs)
 
         ident = held.tile([P, P], F32, name="ident")
-        th_rows = held.tile([P, P], F32, name="th_rows")
+        th_rows = placed.tile([P, P], F32, name="th_rows", offset=TH_HOME)
         warm = held.tile([P, 1], F32, name="warm")
         cs_all = held.tile([P, PAGES], U8, name="cs_all")
         ks_all = held.tile([P, PAGES], U8, name="ks_all")
@@ -78,9 +78,9 @@ def tile_attend_at_quest_topk_kernel(tc, qT, k_words, k_scales, c_words, c_scale
             queue.dma_start(out=cs_all[C_PLANE + r:P:QUADRANT, :].bitcast(I32),
                             in_=c_scales[0, r:SCALE_ROWS:4, :].bitcast(I32))
         nc.sync.dma_start(out=q_raw[1][:], in_=q_rows[:, 2:4, :])
-        nc.sync.dma_start(out=th_rows[0:QB, :], in_=th[0, 0].rearrange("(c p) -> c p", p=P))
         cw_all = placed.tile([P, PAGES], I32, name="cw_all", offset=CW_HOME)
         nc.sync.dma_start(out=cw_all[:], in_=c_words[0].rearrange("p n t -> p (n t)").bitcast(I32))
+        nc.sync.dma_start(out=th_rows[0:QB, :], in_=th[0, 0].rearrange("(c p) -> c p", p=P))
         for r in range(4):
             nc.sync.dma_start(out=ks_all[r:P:QUADRANT, :].bitcast(I32),
                               in_=k_scales[0, r:SCALE_ROWS:4, :].bitcast(I32))
@@ -112,17 +112,17 @@ def tile_attend_at_quest_topk_kernel(tc, qT, k_words, k_scales, c_words, c_scale
         hi_codes = held.tile([P, NQ], U32, name="hi_codes", align_bytes=64)
         hi_scales = held.tile([P, NQ], U8, name="hi_scales", align_bytes=64)
         quantise(hi_codes[:], hi_scales[:], hi_bf[:].rearrange("p q j -> p (q j)"))
-        cw_g = held.tile([P, SLOTS], U32, name="cw_g", align_bytes=64)
+        th_ps = psum.tile([P, P], F32, name="th_ps", offset=TH_BANK * BANK)
+        nc.tensor.transpose(th_ps[:], th_rows[:], ident[:])
+        neg_th = held.tile([P, QB], F32, name="neg_th")
+        nc.scalar.activation(out=neg_th[:], in_=th_ps[:, 0:QB], func=ACT.Copy, scale=-1.0)
+        cw_g = placed.tile([P, SLOTS], U32, name="cw_g", offset=TH_HOME, align_bytes=64)
         nc.vector.tensor_copy(out=cw_g[:], in_=cw_all[:].bitcast(U32).indirect(offsets[:]))
         ks_g = held.tile([P, SLOTS], U8, name="ks_g", align_bytes=64)
         nc.vector.tensor_copy(out=ks_g[:], in_=ks_all[:].indirect(offsets[:]))
         kw_g = held.tile([P, SLOTS], U32, name="kw_g", align_bytes=64)
         nc.vector.tensor_copy(out=kw_g[:], in_=kw_all[:].bitcast(U32).indirect(offsets[:]))
 
-        th_ps = psum.tile([P, P], F32, name="th_ps", offset=TH_BANK * BANK)
-        nc.tensor.transpose(th_ps[:], th_rows[:], ident[:])
-        neg_th = held.tile([P, QB], F32, name="neg_th")
-        nc.scalar.activation(out=neg_th[:], in_=th_ps[:, 0:QB], func=ACT.Copy, scale=-1.0)
         us_laid = held.tile([P, P, PACK], F32, name="us_laid")
         nc.scalar.copy(out=us_laid[:], in_=us_col[:].unsqueeze(1).to_broadcast([P, P, PACK]))
 
@@ -211,8 +211,8 @@ def tile_attend_at_quest_topk_kernel(tc, qT, k_words, k_scales, c_words, c_scale
         v_words = [held.tile([P, P, 2], F32, name=f"v_words{a}", align_bytes=64) for a in range(2)]
         v_words.extend(placed.tile([P, P, 2], F32, name=f"v_words{a}", offset=V_HOME + (22 + 2 * (a - 1)) * KB, align_bytes=64)
                        for a in range(2, EB))
-        lay_values(v_words[0][:], turn_values(0), nc.vector.tensor_copy)
         quantise_gates(1)
+        lay_values(v_words[0][:], turn_values(0), nc.vector.tensor_copy)
         gather_on_scalar(1, 0, SLOTS)
         v_ps1 = turn_values(1)
         operand0 = quantise_values("0", v_words[0][:], V_HOME + 8 * KB)
@@ -223,12 +223,13 @@ def tile_attend_at_quest_topk_kernel(tc, qT, k_words, k_scales, c_words, c_scale
         gather_on_vector(3, 0, LAST_SPLIT)
         gather_on_scalar(3, LAST_SPLIT, SLOTS)
         v_ps3 = turn_values(3)
-        lay_values(v_words[2][:], v_ps2, nc.vector.tensor_copy)
-        multiply(0, operand0, every_block, OUT_BANK[0], nc.scalar.copy, nc.sync, V_HOME + 28 * KB)
+        lay_values(v_words[2][:], v_ps2, nc.scalar.copy)
+        multiply(0, operand0, every_block, OUT_BANK[0], nc.vector.tensor_copy, nc.sync, V_HOME + 28 * KB)
         operand2 = quantise_values("2", v_words[2][:], Q_HOME + KB)
-        multiply(P, operand1, every_block, OUT_BANK[1], nc.vector.tensor_copy, nc.sync, V_HOME + 24 * KB)
+        multiply(P, operand1, every_block, OUT_BANK[1], nc.scalar.copy, nc.sync, V_HOME + 30 * KB)
         lay_values(v_words[3][:], v_ps3, nc.scalar.copy)
         last = quantise_values("3", v_words[3][:], Q_HOME + 3 * KB // 2)
-        multiply(2 * P, operand2, every_block, OUT_BANK[2], nc.scalar.copy, nc.sync, Q_HOME + 2 * KB)
-        multiply(3 * P, last, every_block[:2], LAST_OUT_BANK[0], nc.scalar.copy, nc.scalar, Q_HOME + 4 * KB)
-        multiply(3 * P, last, every_block[2:], LAST_OUT_BANK[1], nc.vector.tensor_copy, nc.sync, Q_HOME + 6 * KB)
+        multiply(2 * P, operand2, every_block[:2], OUT_BANK[2], nc.scalar.copy, nc.sync, Q_HOME + 2 * KB)
+        multiply(2 * P, operand2, every_block[2:], OUT_BANK[3], nc.scalar.copy, nc.sync, Q_HOME + 3 * KB)
+        multiply(3 * P, last, every_block[:2], LAST_OUT_BANK[0], nc.vector.tensor_copy, nc.sync, Q_HOME + 4 * KB)
+        multiply(3 * P, last, every_block[2:], LAST_OUT_BANK[1], nc.scalar.copy, nc.scalar, Q_HOME + 6 * KB)

@@ -49,12 +49,12 @@ def tile_attend_at_quest_topk_kernel(tc, qT, k_words, k_scales, c_words, c_scale
         def quantise(codes, scales, values):
             nc.vector.quantize_mx(out=codes.bitcast(FP8X4), scales=scales, in_=values)
 
+        offsets = held.tile([P, SLOTS // 16], U16, name="offsets")
+        nc.sync.dma_start(offsets[:], offs)
         q_rows = qT[0].rearrange("(p j) q -> p j q", j=PACK)
         q_raw = [held.tile([P, 2, NQ], F32, name="q_raw0"),
                  placed.tile([P, 2, NQ], F32, name="q_raw1", offset=Q_HOME)]
         nc.sync.dma_start(out=q_raw[0][:], in_=q_rows[:, 0:2, :])
-        offsets = held.tile([P, SLOTS // 16], U16, name="offsets")
-        nc.sync.dma_start(offsets[:], offs)
 
         ident = held.tile([P, P], F32, name="ident")
         th_rows = placed.tile([P, P], F32, name="th_rows", offset=TH_HOME)
@@ -74,13 +74,12 @@ def tile_attend_at_quest_topk_kernel(tc, qT, k_words, k_scales, c_words, c_scale
                                 pattern=[[-1, P]], channel_multiplier=1)
 
         for r in range(4):
-            queue = nc.sync if r < 2 else nc.scalar
-            queue.dma_start(out=cs_all[C_PLANE + r:P:QUADRANT, :].bitcast(I32),
-                            in_=c_scales[0, r:SCALE_ROWS:4, :].bitcast(I32))
+            nc.sync.dma_start(out=cs_all[C_PLANE + r:P:QUADRANT, :].bitcast(I32),
+                              in_=c_scales[0, r:SCALE_ROWS:4, :].bitcast(I32))
         nc.sync.dma_start(out=q_raw[1][:], in_=q_rows[:, 2:4, :])
+        nc.sync.dma_start(out=th_rows[0:QB, :], in_=th[0, 0].rearrange("(c p) -> c p", p=P))
         cw_all = placed.tile([P, PAGES], I32, name="cw_all", offset=CW_HOME)
         nc.sync.dma_start(out=cw_all[:], in_=c_words[0].rearrange("p n t -> p (n t)").bitcast(I32))
-        nc.sync.dma_start(out=th_rows[0:QB, :], in_=th[0, 0].rearrange("(c p) -> c p", p=P))
         for r in range(4):
             nc.sync.dma_start(out=ks_all[r:P:QUADRANT, :].bitcast(I32),
                               in_=k_scales[0, r:SCALE_ROWS:4, :].bitcast(I32))
@@ -99,19 +98,28 @@ def tile_attend_at_quest_topk_kernel(tc, qT, k_words, k_scales, c_words, c_scale
 
         def split_queries(u):
             source = q_raw[u][:].rearrange("p e q -> p q e")
-            nc.scalar.activation(out=hi_bf[:, :, 2 * u:2 * u + 2], in_=source, func=ACT.Relu)
+            for h in range(2):
+                cols = slice(h * HALF, (h + 1) * HALF)
+                nc.scalar.activation(out=hi_bf[:, cols, 2 * u:2 * u + 2], in_=source[:, cols, :], func=ACT.Relu)
             nc.vector.tensor_scalar_min(out=lo_bf[:, :, 2 * u:2 * u + 2], in0=source, scalar1=0.0)
 
         split_queries(0)
         cs_g = held.tile([P, SLOTS], U8, name="cs_g", align_bytes=64)
         nc.vector.tensor_copy(out=cs_g[:], in_=cs_all[:].indirect(offsets[:]))
         split_queries(1)
-        lo_codes = held.tile([P, NQ], U32, name="lo_codes", align_bytes=64)
-        lo_scales = held.tile([P, NQ], U8, name="lo_scales", align_bytes=64)
-        quantise(lo_codes[:], lo_scales[:], lo_bf[:].rearrange("p q j -> p (q j)"))
-        hi_codes = held.tile([P, NQ], U32, name="hi_codes", align_bytes=64)
-        hi_scales = held.tile([P, NQ], U8, name="hi_scales", align_bytes=64)
-        quantise(hi_codes[:], hi_scales[:], hi_bf[:].rearrange("p q j -> p (q j)"))
+        lo_codes = [held.tile([P, HALF], U32, name="lo_codes0", align_bytes=64),
+                    placed.tile([P, HALF], U32, name="lo_codes1", offset=KW_HOME, align_bytes=64)]
+        hi_codes = [held.tile([P, HALF], U32, name="hi_codes0", align_bytes=64),
+                    placed.tile([P, HALF], U32, name="hi_codes1", offset=KW_HOME + KB, align_bytes=64)]
+        lo_scales = [held.tile([P, HALF], U8, name=f"lo_scales{h}", align_bytes=64) for h in range(2)]
+        hi_scales = [held.tile([P, HALF], U8, name=f"hi_scales{h}", align_bytes=64) for h in range(2)]
+
+        def quantise_queries(h):
+            cols = slice(h * HALF, (h + 1) * HALF)
+            quantise(lo_codes[h][:], lo_scales[h][:], lo_bf[:, cols, :].rearrange("p q j -> p (q j)"))
+            quantise(hi_codes[h][:], hi_scales[h][:], hi_bf[:, cols, :].rearrange("p q j -> p (q j)"))
+
+        quantise_queries(0)
         th_ps = psum.tile([P, P], F32, name="th_ps", offset=TH_BANK * BANK)
         nc.tensor.transpose(th_ps[:], th_rows[:], ident[:])
         neg_th = held.tile([P, QB], F32, name="neg_th")
@@ -122,19 +130,26 @@ def tile_attend_at_quest_topk_kernel(tc, qT, k_words, k_scales, c_words, c_scale
         nc.vector.tensor_copy(out=ks_g[:], in_=ks_all[:].indirect(offsets[:]))
         kw_g = held.tile([P, SLOTS], U32, name="kw_g", align_bytes=64)
         nc.vector.tensor_copy(out=kw_g[:], in_=kw_all[:].bitcast(U32).indirect(offsets[:]))
+        quantise_queries(1)
 
         us_laid = held.tile([P, P, PACK], F32, name="us_laid")
         nc.scalar.copy(out=us_laid[:], in_=us_col[:].unsqueeze(1).to_broadcast([P, P, PACK]))
 
         scores = [psum.tile([P, SLOTS], F32, name=f"score{c}", offset=c * BANK) for c in range(QB)]
-        for c in range(QB):
-            cols = slice(c * P, (c + 1) * P)
-            nc.tensor.matmul_mx(out=scores[c][:], lhsT=lo_codes[:, cols].bitcast(FP8X4), lhsT_scale=lo_scales[:, cols],
-                                rhs=cw_g[:].bitcast(FP8X4), rhs_scale=cs_g[C_PLANE:P, :], start=True, stop=False)
-        for c in range(QB):
-            cols = slice(c * P, (c + 1) * P)
-            nc.tensor.matmul_mx(out=scores[c][:], lhsT=hi_codes[:, cols].bitcast(FP8X4), lhsT_scale=hi_scales[:, cols],
-                                rhs=kw_g[:].bitcast(FP8X4), rhs_scale=ks_g[:], start=False, stop=True)
+
+        def score(c, codes, scales, words, word_scales, first):
+            cols = slice(c % 2 * P, (c % 2 + 1) * P)
+            nc.tensor.matmul_mx(out=scores[c][:], lhsT=codes[c // 2][:, cols].bitcast(FP8X4),
+                                lhsT_scale=scales[c // 2][:, cols], rhs=words[:].bitcast(FP8X4), rhs_scale=word_scales,
+                                start=first, stop=not first)
+
+        for c in range(2):
+            score(c, lo_codes, lo_scales, cw_g, cs_g[C_PLANE:P, :], True)
+        for c in range(2):
+            score(c, hi_codes, hi_scales, kw_g, ks_g[:], False)
+        for c in range(2, QB):
+            score(c, lo_codes, lo_scales, cw_g, cs_g[C_PLANE:P, :], True)
+            score(c, hi_codes, hi_scales, kw_g, ks_g[:], False)
 
         out_rows = out[0].rearrange("(c p) e -> p c e", p=P)
         y_bf = [placed.tile([P, HALF, PACK], BF16, name=f"y_bf{h}", offset=V_HOME + h * 2 * KB, align_bytes=64)

@@ -49,12 +49,12 @@ def tile_attend_at_quest_topk_kernel(tc, qT, k_words, k_scales, c_words, c_scale
         def quantise(codes, scales, values):
             nc.vector.quantize_mx(out=codes.bitcast(FP8X4), scales=scales, in_=values)
 
-        offsets = held.tile([P, SLOTS // 16], U16, name="offsets")
-        nc.sync.dma_start(offsets[:], offs)
         q_rows = qT[0].rearrange("(p j) q -> p j q", j=PACK)
         q_raw = [held.tile([P, 2, NQ], F32, name="q_raw0"),
                  placed.tile([P, 2, NQ], F32, name="q_raw1", offset=Q_HOME)]
         nc.sync.dma_start(out=q_raw[0][:], in_=q_rows[:, 0:2, :])
+        offsets = held.tile([P, SLOTS // 16], U16, name="offsets")
+        nc.sync.dma_start(offsets[:], offs)
 
         ident = held.tile([P, P], F32, name="ident")
         th_rows = placed.tile([P, P], F32, name="th_rows", offset=TH_HOME)
@@ -77,9 +77,9 @@ def tile_attend_at_quest_topk_kernel(tc, qT, k_words, k_scales, c_words, c_scale
             nc.sync.dma_start(out=cs_all[C_PLANE + r:P:QUADRANT, :].bitcast(I32),
                               in_=c_scales[0, r:SCALE_ROWS:4, :].bitcast(I32))
         nc.sync.dma_start(out=q_raw[1][:], in_=q_rows[:, 2:4, :])
-        nc.sync.dma_start(out=th_rows[0:QB, :], in_=th[0, 0].rearrange("(c p) -> c p", p=P))
         cw_all = placed.tile([P, PAGES], I32, name="cw_all", offset=CW_HOME)
         nc.sync.dma_start(out=cw_all[:], in_=c_words[0].rearrange("p n t -> p (n t)").bitcast(I32))
+        nc.sync.dma_start(out=th_rows[0:QB, :], in_=th[0, 0].rearrange("(c p) -> c p", p=P))
         for r in range(4):
             nc.sync.dma_start(out=ks_all[r:P:QUADRANT, :].bitcast(I32),
                               in_=k_scales[0, r:SCALE_ROWS:4, :].bitcast(I32))
@@ -107,19 +107,18 @@ def tile_attend_at_quest_topk_kernel(tc, qT, k_words, k_scales, c_words, c_scale
         cs_g = held.tile([P, SLOTS], U8, name="cs_g", align_bytes=64)
         nc.vector.tensor_copy(out=cs_g[:], in_=cs_all[:].indirect(offsets[:]))
         split_queries(1)
-        lo_codes = [held.tile([P, HALF], U32, name="lo_codes0", align_bytes=64),
-                    placed.tile([P, HALF], U32, name="lo_codes1", offset=KW_HOME, align_bytes=64)]
+        lo_codes = held.tile([P, NQ], U32, name="lo_codes", align_bytes=64)
+        lo_scales = held.tile([P, NQ], U8, name="lo_scales", align_bytes=64)
+        quantise(lo_codes[:], lo_scales[:], lo_bf[:].rearrange("p q j -> p (q j)"))
         hi_codes = [held.tile([P, HALF], U32, name="hi_codes0", align_bytes=64),
-                    placed.tile([P, HALF], U32, name="hi_codes1", offset=KW_HOME + KB, align_bytes=64)]
-        lo_scales = [held.tile([P, HALF], U8, name=f"lo_scales{h}", align_bytes=64) for h in range(2)]
+                    placed.tile([P, HALF], U32, name="hi_codes1", offset=KW_HOME, align_bytes=64)]
         hi_scales = [held.tile([P, HALF], U8, name=f"hi_scales{h}", align_bytes=64) for h in range(2)]
 
-        def quantise_queries(h):
+        def quantise_high(h):
             cols = slice(h * HALF, (h + 1) * HALF)
-            quantise(lo_codes[h][:], lo_scales[h][:], lo_bf[:, cols, :].rearrange("p q j -> p (q j)"))
             quantise(hi_codes[h][:], hi_scales[h][:], hi_bf[:, cols, :].rearrange("p q j -> p (q j)"))
 
-        quantise_queries(0)
+        quantise_high(0)
         th_ps = psum.tile([P, P], F32, name="th_ps", offset=TH_BANK * BANK)
         nc.tensor.transpose(th_ps[:], th_rows[:], ident[:])
         neg_th = held.tile([P, QB], F32, name="neg_th")
@@ -130,26 +129,21 @@ def tile_attend_at_quest_topk_kernel(tc, qT, k_words, k_scales, c_words, c_scale
         nc.vector.tensor_copy(out=ks_g[:], in_=ks_all[:].indirect(offsets[:]))
         kw_g = held.tile([P, SLOTS], U32, name="kw_g", align_bytes=64)
         nc.vector.tensor_copy(out=kw_g[:], in_=kw_all[:].bitcast(U32).indirect(offsets[:]))
-        quantise_queries(1)
+        quantise_high(1)
 
         us_laid = held.tile([P, P, PACK], F32, name="us_laid")
         nc.scalar.copy(out=us_laid[:], in_=us_col[:].unsqueeze(1).to_broadcast([P, P, PACK]))
 
         scores = [psum.tile([P, SLOTS], F32, name=f"score{c}", offset=c * BANK) for c in range(QB)]
-
-        def score(c, codes, scales, words, word_scales, first):
+        for c in range(QB):
+            cols = slice(c * P, (c + 1) * P)
+            nc.tensor.matmul_mx(out=scores[c][:], lhsT=lo_codes[:, cols].bitcast(FP8X4), lhsT_scale=lo_scales[:, cols],
+                                rhs=cw_g[:].bitcast(FP8X4), rhs_scale=cs_g[C_PLANE:P, :], start=True, stop=False)
+        for c in range(QB):
             cols = slice(c % 2 * P, (c % 2 + 1) * P)
-            nc.tensor.matmul_mx(out=scores[c][:], lhsT=codes[c // 2][:, cols].bitcast(FP8X4),
-                                lhsT_scale=scales[c // 2][:, cols], rhs=words[:].bitcast(FP8X4), rhs_scale=word_scales,
-                                start=first, stop=not first)
-
-        for c in range(2):
-            score(c, lo_codes, lo_scales, cw_g, cs_g[C_PLANE:P, :], True)
-        for c in range(2):
-            score(c, hi_codes, hi_scales, kw_g, ks_g[:], False)
-        for c in range(2, QB):
-            score(c, lo_codes, lo_scales, cw_g, cs_g[C_PLANE:P, :], True)
-            score(c, hi_codes, hi_scales, kw_g, ks_g[:], False)
+            nc.tensor.matmul_mx(out=scores[c][:], lhsT=hi_codes[c // 2][:, cols].bitcast(FP8X4),
+                                lhsT_scale=hi_scales[c // 2][:, cols],
+                                rhs=kw_g[:].bitcast(FP8X4), rhs_scale=ks_g[:], start=False, stop=True)
 
         out_rows = out[0].rearrange("(c p) e -> p c e", p=P)
         y_bf = [placed.tile([P, HALF, PACK], BF16, name=f"y_bf{h}", offset=V_HOME + h * 2 * KB, align_bytes=64)

@@ -20,16 +20,19 @@ EB = DV // P
 HALF = NQ // 2
 RUN = 4
 SCALE_ROWS, QUADRANT = 16, 32
-C_PLANE = 4
 
 KB = 1024
 Q_HOME, CW_HOME, KW_HOME = 0, 8 * KB, 16 * KB
-V_HOME = 24 * KB
-US_HOME = 56 * KB
-LATE_END = US_HOME + 32
-
-TH_HOME = 57 * KB
+US_HOME = 24 * KB
+EARLY_END = US_HOME + 32
+V_HOME = 26 * KB
+TH_HOME = 59 * KB
+CS_HOME, LOW_HOME = 60 * KB, 62 * KB
+FIRST_SPLIT = 384
+THIRD_SPLIT = 128
+ROW_FIRST, ROW_STEP = 32, 4
 LAST_SPLIT = 288
+LAST_GATHER_HOME = Q_HOME + 7 * KB
 BANK = 2048
 TH_BANK = 7
 V_TURN_BANK = (1, 5, 6, 7)
@@ -50,110 +53,126 @@ def tile_attend_at_quest_topk_kernel(tc, qT, k_words, k_scales, c_words, c_scale
             nc.vector.quantize_mx(out=codes.bitcast(FP8X4), scales=scales, in_=values)
 
         q_rows = qT[0].rearrange("(p j) q -> p j q", j=PACK)
-        q_raw = [held.tile([P, 2, NQ], F32, name="q_raw0"),
-                 placed.tile([P, 2, NQ], F32, name="q_raw1", offset=Q_HOME)]
-        nc.sync.dma_start(out=q_raw[0][:], in_=q_rows[:, 0:2, :])
+        q_raw = [held.tile([P, PACK, HALF], F32, name="q_raw0"),
+                 placed.tile([P, PACK, HALF], F32, name="q_raw1", offset=Q_HOME)]
+        nc.sync.dma_start(out=q_raw[0][:], in_=q_rows[:, :, 0:HALF])
         offsets = held.tile([P, SLOTS // 16], U16, name="offsets")
         nc.sync.dma_start(offsets[:], offs)
 
         ident = held.tile([P, P], F32, name="ident")
         th_rows = placed.tile([P, P], F32, name="th_rows", offset=TH_HOME)
         warm = held.tile([P, 1], F32, name="warm")
-        cs_all = held.tile([P, PAGES], U8, name="cs_all")
-        ks_all = held.tile([P, PAGES], U8, name="ks_all")
-        zeros_a = placed.tile([P, (KW_HOME - Q_HOME) // 4], F32, name="zeros_a", offset=Q_HOME)
-        zeros_b = placed.tile([P, (LATE_END - KW_HOME) // 4], F32, name="zeros_b", offset=KW_HOME)
-        nc.vector.memset(warm[:], 0.0)
+        cs_all = placed.tile([P, PAGES], U8, name="cs_all", offset=CS_HOME)
+        ks_all = placed.tile([P, EB * 8 * KB], U8, name="ks_all", offset=V_HOME)
+        planes = held.tile([P, 2 * SLOTS], U8, name="planes", align_bytes=64)
+        zeros = placed.tile([P, (EARLY_END - Q_HOME) // 4], F32, name="zeros", offset=Q_HOME)
+        nc.gpsimd.memset(warm[:], 0.0)
         nc.scalar.activation(out=warm[:], in_=warm[:], func=ACT.Sigmoid)
-        nc.gpsimd.memset(zeros_a[:, 0:P], 0.0)
-        nc.gpsimd.memset(cs_all[:].bitcast(I32), 0)
-        nc.gpsimd.tensor_copy(out=th_rows[:], in_=zeros_a[:, 0:P])
-        nc.gpsimd.memset(zeros_b[:, 0:P], 0.0)
-        nc.gpsimd.memset(ks_all[:].bitcast(I32), 0)
-        nc.gpsimd.affine_select(out=ident[:], in_=zeros_b[:, 0:P], compare_op=ALU.not_equal, fill=1.0, base=0,
+        nc.gpsimd.memset(zeros[:, 0:P], 0.0)
+        nc.vector.memset(cs_all[:].bitcast(I32), 0)
+        nc.vector.memset(ks_all[:, 0:PAGES].bitcast(I32), 0)
+        nc.vector.tensor_copy(out=th_rows[:], in_=zeros[:, 0:P])
+        nc.gpsimd.memset(ident[:], 0.0)
+        nc.gpsimd.affine_select(out=ident[:], in_=ident[:], compare_op=ALU.not_equal, fill=1.0, base=0,
                                 pattern=[[-1, P]], channel_multiplier=1)
+        nc.gpsimd.memset(planes[:].bitcast(I32), 0)
 
-        for r in range(4):
-            nc.sync.dma_start(out=cs_all[C_PLANE + r:P:QUADRANT, :].bitcast(I32),
-                              in_=c_scales[0, r:SCALE_ROWS:4, :].bitcast(I32))
-        nc.sync.dma_start(out=q_raw[1][:], in_=q_rows[:, 2:4, :])
+        loaded_rows = slice(ROW_FIRST, ROW_FIRST + ROW_STEP * SCALE_ROWS, ROW_STEP)
+        nc.sync.dma_start(out=cs_all[loaded_rows, :].bitcast(I32), in_=c_scales[0].bitcast(I32))
+        nc.sync.dma_start(out=ks_all[loaded_rows, 0:PAGES].bitcast(I32), in_=k_scales[0].bitcast(I32))
         cw_all = placed.tile([P, PAGES], I32, name="cw_all", offset=CW_HOME)
         nc.sync.dma_start(out=cw_all[:], in_=c_words[0].rearrange("p n t -> p (n t)").bitcast(I32))
         nc.sync.dma_start(out=th_rows[0:QB, :], in_=th[0, 0].rearrange("(c p) -> c p", p=P))
-        for r in range(4):
-            nc.sync.dma_start(out=ks_all[r:P:QUADRANT, :].bitcast(I32),
-                              in_=k_scales[0, r:SCALE_ROWS:4, :].bitcast(I32))
-        kw_all = placed.tile([P, PAGES], I32, name="kw_all", offset=KW_HOME)
-        nc.sync.dma_start(out=kw_all[:], in_=k_words[0].rearrange("p n t -> p (n t)").bitcast(I32))
         us_col = placed.tile([P, PACK], F32, name="us_col", offset=US_HOME)
         nc.sync.dma_start(out=us_col[:], in_=us[0].rearrange("(p t) o -> p (t o)", t=PACK))
+        kw_all = placed.tile([P, PAGES], I32, name="kw_all", offset=KW_HOME)
+        nc.sync.dma_start(out=kw_all[:], in_=k_words[0].rearrange("p n t -> p (n t)").bitcast(I32))
+        nc.sync.dma_start(out=q_raw[1][:], in_=q_rows[:, :, HALF:NQ])
+
+        rows_g = held.tile([P, 2 * SLOTS], U8, name="rows_g", align_bytes=64)
+        nc.vector.tensor_copy(out=rows_g[:, 0:SLOTS], in_=cs_all[:].indirect(offsets[:]))
+        nc.vector.tensor_copy(out=rows_g[:, SLOTS:2 * SLOTS], in_=ks_all[:, 0:PAGES].indirect(offsets[:]))
+        for r in range(4):
+            first = ROW_FIRST + ROW_STEP * r
+            nc.sync.dma_start(out=planes[r:P:QUADRANT, :].bitcast(I32),
+                              in_=rows_g[first:first + 4 * 4 * ROW_STEP:4 * ROW_STEP, :].bitcast(I32))
         v_all = []
         for a in range(EB):
             v_tile = placed.tile([P, PAGES], F32, name=f"v_all{a}", offset=V_HOME + a * 8 * KB)
             nc.sync.dma_start(out=v_tile[:], in_=vT[a * P:(a + 1) * P, :])
             v_all.append(v_tile)
 
-        lo_bf = held.tile([P, NQ, PACK], BF16, name="lo_bf", align_bytes=64)
-        hi_bf = held.tile([P, NQ, PACK], BF16, name="hi_bf", align_bytes=64)
-
-        def split_queries(u):
-            source = q_raw[u][:].rearrange("p e q -> p q e")
-            for h in range(2):
-                cols = slice(h * HALF, (h + 1) * HALF)
-                nc.scalar.activation(out=hi_bf[:, cols, 2 * u:2 * u + 2], in_=source[:, cols, :], func=ACT.Relu)
-            nc.vector.tensor_scalar_min(out=lo_bf[:, :, 2 * u:2 * u + 2], in0=source, scalar1=0.0)
-
-        split_queries(0)
-        cs_g = held.tile([P, SLOTS], U8, name="cs_g", align_bytes=64)
-        nc.vector.tensor_copy(out=cs_g[:], in_=cs_all[:].indirect(offsets[:]))
-        split_queries(1)
-        lo_codes = held.tile([P, NQ], U32, name="lo_codes", align_bytes=64)
-        lo_scales = held.tile([P, NQ], U8, name="lo_scales", align_bytes=64)
-        quantise(lo_codes[:], lo_scales[:], lo_bf[:].rearrange("p q j -> p (q j)"))
-        hi_codes = [held.tile([P, HALF], U32, name="hi_codes0", align_bytes=64),
-                    placed.tile([P, HALF], U32, name="hi_codes1", offset=KW_HOME, align_bytes=64)]
+        q_bf = [held.tile([P, HALF, PACK], BF16, name="q_bf0", align_bytes=64)]
+        lo_bf = [placed.tile([P, HALF, PACK], BF16, name="lo_bf0", offset=CS_HOME, align_bytes=64),
+                 placed.tile([P, HALF, PACK], BF16, name="lo_bf1", offset=LOW_HOME, align_bytes=64)]
+        hi_bf = [held.tile([P, HALF, PACK], BF16, name=f"hi_bf{h}", align_bytes=64) for h in range(2)]
+        lo_codes = [placed.tile([P, HALF], U32, name="lo_codes0", offset=CW_HOME, align_bytes=64),
+                    held.tile([P, HALF], U32, name="lo_codes1", align_bytes=64)]
+        hi_codes = [placed.tile([P, HALF], U32, name="hi_codes0", offset=CW_HOME + KB, align_bytes=64),
+                    held.tile([P, HALF], U32, name="hi_codes1", align_bytes=64)]
+        lo_scales = [held.tile([P, HALF], U8, name=f"lo_scales{h}", align_bytes=64) for h in range(2)]
         hi_scales = [held.tile([P, HALF], U8, name=f"hi_scales{h}", align_bytes=64) for h in range(2)]
 
-        def quantise_high(h):
-            cols = slice(h * HALF, (h + 1) * HALF)
-            quantise(hi_codes[h][:], hi_scales[h][:], hi_bf[:, cols, :].rearrange("p q j -> p (q j)"))
+        def round_queries(h):
+            nc.scalar.copy(out=q_bf[h][:], in_=q_raw[h][:].rearrange("p j q -> p q j"))
 
-        quantise_high(0)
+        def quantise_queries(h):
+            quantise(lo_codes[h][:], lo_scales[h][:], lo_bf[h][:].rearrange("p q j -> p (q j)"))
+            quantise(hi_codes[h][:], hi_scales[h][:], hi_bf[h][:].rearrange("p q j -> p (q j)"))
+
+        round_queries(0)
+        nc.scalar.activation(out=hi_bf[0][:], in_=q_bf[0][:], func=ACT.Relu)
+        nc.vector.tensor_scalar_min(out=lo_bf[0][:], in0=q_bf[0][:], scalar1=0.0)
+        cw_g = held.tile([P, SLOTS], U32, name="cw_g", align_bytes=64)
+        nc.vector.tensor_copy(out=cw_g[:], in_=cw_all[:].bitcast(U32).indirect(offsets[:]))
+        quantise_queries(0)
+        kw_g = held.tile([P, SLOTS], U32, name="kw_g", align_bytes=64)
+        nc.vector.tensor_copy(out=kw_g[:], in_=kw_all[:].bitcast(U32).indirect(offsets[:]))
+
         th_ps = psum.tile([P, P], F32, name="th_ps", offset=TH_BANK * BANK)
         nc.tensor.transpose(th_ps[:], th_rows[:], ident[:])
         neg_th = held.tile([P, QB], F32, name="neg_th")
         nc.scalar.activation(out=neg_th[:], in_=th_ps[:, 0:QB], func=ACT.Copy, scale=-1.0)
-        cw_g = placed.tile([P, SLOTS], U32, name="cw_g", offset=TH_HOME, align_bytes=64)
-        nc.vector.tensor_copy(out=cw_g[:], in_=cw_all[:].bitcast(U32).indirect(offsets[:]))
-        ks_g = held.tile([P, SLOTS], U8, name="ks_g", align_bytes=64)
-        nc.vector.tensor_copy(out=ks_g[:], in_=ks_all[:].indirect(offsets[:]))
-        kw_g = held.tile([P, SLOTS], U32, name="kw_g", align_bytes=64)
-        nc.vector.tensor_copy(out=kw_g[:], in_=kw_all[:].bitcast(U32).indirect(offsets[:]))
-        quantise_high(1)
-
         us_laid = held.tile([P, P, PACK], F32, name="us_laid")
         nc.scalar.copy(out=us_laid[:], in_=us_col[:].unsqueeze(1).to_broadcast([P, P, PACK]))
 
+        second = q_raw[1][:].rearrange("p j q -> p q j")
+        nc.scalar.activation(out=hi_bf[1][:], in_=second, func=ACT.Relu)
+        nc.vector.tensor_scalar_min(out=lo_bf[1][:], in0=second, scalar1=0.0)
+        quantise_queries(1)
+
+        idle_ps = psum.tile([P, SLOTS], F32, name="idle_ps", offset=TH_BANK * BANK)
+        for c in range(2):
+            nc.tensor.matmul_mx(out=idle_ps[:], lhsT=cw_g[:, c * P:(c + 1) * P].bitcast(FP8X4),
+                                lhsT_scale=rows_g[:, c * P:(c + 1) * P], rhs=cw_g[:].bitcast(FP8X4),
+                                rhs_scale=rows_g[:, 0:SLOTS], start=True, stop=True)
+
         scores = [psum.tile([P, SLOTS], F32, name=f"score{c}", offset=c * BANK) for c in range(QB)]
-        for c in range(QB):
-            cols = slice(c * P, (c + 1) * P)
-            nc.tensor.matmul_mx(out=scores[c][:], lhsT=lo_codes[:, cols].bitcast(FP8X4), lhsT_scale=lo_scales[:, cols],
-                                rhs=cw_g[:].bitcast(FP8X4), rhs_scale=cs_g[C_PLANE:P, :], start=True, stop=False)
-        for c in range(QB):
+
+        def score_pass(c, codes, scales, keys, plane, first):
             cols = slice(c % 2 * P, (c % 2 + 1) * P)
-            nc.tensor.matmul_mx(out=scores[c][:], lhsT=hi_codes[c // 2][:, cols].bitcast(FP8X4),
-                                lhsT_scale=hi_scales[c // 2][:, cols],
-                                rhs=kw_g[:].bitcast(FP8X4), rhs_scale=ks_g[:], start=False, stop=True)
+            nc.tensor.matmul_mx(out=scores[c][:], lhsT=codes[c // 2][:, cols].bitcast(FP8X4),
+                                lhsT_scale=scales[c // 2][:, cols], rhs=keys[:].bitcast(FP8X4), rhs_scale=plane,
+                                start=first, stop=not first)
+
+        for c in range(QB):
+            score_pass(c, lo_codes, lo_scales, cw_g, planes[:, 0:SLOTS], True)
+            score_pass(c, hi_codes, hi_scales, kw_g, planes[:, SLOTS:2 * SLOTS], False)
 
         out_rows = out[0].rearrange("(c p) e -> p c e", p=P)
         y_bf = [placed.tile([P, HALF, PACK], BF16, name=f"y_bf{h}", offset=V_HOME + h * 2 * KB, align_bytes=64)
                 for h in range(2)]
         y_codes = [held.tile([P, HALF], U32, name=f"y_codes{h}", align_bytes=64) for h in range(2)]
         y_scales = [held.tile([P, HALF], U8, name=f"y_scales{h}", align_bytes=64) for h in range(2)]
-        v_g = [held.tile([P, SLOTS], BF16, name=f"v_g{a}") for a in range(EB)]
+        v_g = [placed.tile([P, SLOTS], BF16, name="v_g0", offset=LOW_HOME),
+               held.tile([P, SLOTS], BF16, name="v_g1"), held.tile([P, SLOTS], BF16, name="v_g2"),
+               placed.tile([P, SLOTS], BF16, name="v_g3", offset=LAST_GATHER_HOME)]
 
         def gate(c):
-            sig = held.tile([P, PACK, P], F32, name=f"sig{c}")
+            if c >= 2:
+                sig = placed.tile([P, PACK, P], F32, name=f"sig{c}", offset=V_HOME + 2 * c * KB)
+            else:
+                sig = held.tile([P, PACK, P], F32, name=f"sig{c}")
             nc.scalar.activation(out=sig[:], in_=scores[c][:].rearrange("q (s t) -> q t s", t=PACK),
                                  func=ACT.Sigmoid, bias=neg_th[:, c:c + 1])
             return sig
@@ -210,8 +229,10 @@ def tile_attend_at_quest_topk_kernel(tc, qT, k_words, k_scales, c_words, c_scale
             queue.dma_start(out=out_rows[:, blocks[0]:blocks[-1] + 1, first:first + width], in_=result[:])
 
         every_block = list(range(QB))
-        sigs = [gate(c) for c in range(QB)]
-        gather_on_vector(0, 0, SLOTS)
+        sigs = [gate(0), gate(1)]
+        gather_on_vector(0, 0, FIRST_SPLIT)
+        gather_on_scalar(0, FIRST_SPLIT, SLOTS)
+        sigs.extend([gate(2), gate(3)])
         turned = [turn_gate(c, sigs[c]) for c in range(QB)]
         for c in range(QB - 1):
             scale_gate(c, turned[c])
@@ -226,7 +247,8 @@ def tile_attend_at_quest_topk_kernel(tc, qT, k_words, k_scales, c_words, c_scale
         v_ps1 = turn_values(1)
         operand0 = quantise_values("0", v_words[0][:], V_HOME + 8 * KB)
         lay_values(v_words[1][:], v_ps1, nc.vector.tensor_copy)
-        gather_on_scalar(2, 0, SLOTS)
+        gather_on_vector(2, 0, THIRD_SPLIT)
+        gather_on_scalar(2, THIRD_SPLIT, SLOTS)
         v_ps2 = turn_values(2)
         operand1 = quantise_values("1", v_words[1][:], V_HOME + 16 * KB)
         gather_on_vector(3, 0, LAST_SPLIT)
@@ -235,8 +257,9 @@ def tile_attend_at_quest_topk_kernel(tc, qT, k_words, k_scales, c_words, c_scale
         lay_values(v_words[2][:], v_ps2, nc.scalar.copy)
         multiply(0, operand0, every_block, OUT_BANK[0], nc.vector.tensor_copy, nc.sync, V_HOME + 28 * KB)
         operand2 = quantise_values("2", v_words[2][:], Q_HOME + KB)
-        multiply(P, operand1, every_block, OUT_BANK[1], nc.scalar.copy, nc.sync, V_HOME + 30 * KB)
+        multiply(P, operand1, every_block[:2], OUT_BANK[1], nc.scalar.copy, nc.sync, V_HOME + 30 * KB)
         lay_values(v_words[3][:], v_ps3, nc.scalar.copy)
+        multiply(P, operand1, every_block[2:], V_TURN_BANK[2], nc.scalar.copy, nc.sync, LAST_GATHER_HOME)
         last = quantise_values("3", v_words[3][:], Q_HOME + 3 * KB // 2)
         multiply(2 * P, operand2, every_block[:2], OUT_BANK[2], nc.scalar.copy, nc.sync, Q_HOME + 2 * KB)
         multiply(2 * P, operand2, every_block[2:], OUT_BANK[3], nc.scalar.copy, nc.sync, Q_HOME + 3 * KB)

@@ -28,7 +28,6 @@ EARLY_END = US_HOME + 32
 V_HOME = 26 * KB
 TH_HOME = 59 * KB
 CS_HOME, LOW_HOME = 60 * KB, 62 * KB
-FIRST_SPLIT = 384
 THIRD_SPLIT = 128
 ROW_FIRST, ROW_STEP = 32, 4
 LAST_SPLIT = 288
@@ -104,8 +103,9 @@ def tile_attend_at_quest_topk_kernel(tc, qT, k_words, k_scales, c_words, c_scale
 
         q_bf = [held.tile([P, HALF, PACK], BF16, name="q_bf0", align_bytes=64)]
         lo_bf = [placed.tile([P, HALF, PACK], BF16, name="lo_bf0", offset=CS_HOME, align_bytes=64),
-                 placed.tile([P, HALF, PACK], BF16, name="lo_bf1", offset=LOW_HOME, align_bytes=64)]
-        hi_bf = [held.tile([P, HALF, PACK], BF16, name=f"hi_bf{h}", align_bytes=64) for h in range(2)]
+                 held.tile([P, HALF, PACK], BF16, name="lo_bf1", align_bytes=64)]
+        hi_bf = [held.tile([P, HALF, PACK], BF16, name="hi_bf0", align_bytes=64),
+                 placed.tile([P, HALF, PACK], BF16, name="hi_bf1", offset=LOW_HOME, align_bytes=64)]
         lo_codes = [placed.tile([P, HALF], U32, name="lo_codes0", offset=CW_HOME, align_bytes=64),
                     held.tile([P, HALF], U32, name="lo_codes1", align_bytes=64)]
         hi_codes = [placed.tile([P, HALF], U32, name="hi_codes0", offset=CW_HOME + KB, align_bytes=64),
@@ -169,10 +169,7 @@ def tile_attend_at_quest_topk_kernel(tc, qT, k_words, k_scales, c_words, c_scale
                placed.tile([P, SLOTS], BF16, name="v_g3", offset=LAST_GATHER_HOME)]
 
         def gate(c):
-            if c >= 2:
-                sig = placed.tile([P, PACK, P], F32, name=f"sig{c}", offset=V_HOME + 2 * c * KB)
-            else:
-                sig = held.tile([P, PACK, P], F32, name=f"sig{c}")
+            sig = held.tile([P, PACK, P], F32, name=f"sig{c}")
             nc.scalar.activation(out=sig[:], in_=scores[c][:].rearrange("q (s t) -> q t s", t=PACK),
                                  func=ACT.Sigmoid, bias=neg_th[:, c:c + 1])
             return sig
@@ -229,10 +226,8 @@ def tile_attend_at_quest_topk_kernel(tc, qT, k_words, k_scales, c_words, c_scale
             queue.dma_start(out=out_rows[:, blocks[0]:blocks[-1] + 1, first:first + width], in_=result[:])
 
         every_block = list(range(QB))
-        sigs = [gate(0), gate(1)]
-        gather_on_vector(0, 0, FIRST_SPLIT)
-        gather_on_scalar(0, FIRST_SPLIT, SLOTS)
-        sigs.extend([gate(2), gate(3)])
+        sigs = [gate(c) for c in range(QB)]
+        gather_on_vector(0, 0, SLOTS)
         turned = [turn_gate(c, sigs[c]) for c in range(QB)]
         for c in range(QB - 1):
             scale_gate(c, turned[c])

from contextlib import ExitStack

import concourse.mybir as mybir

F32 = mybir.dt.float32
BF16 = mybir.dt.bfloat16
I32 = mybir.dt.int32
U32 = mybir.dt.uint32
U16 = mybir.dt.uint16
U8 = mybir.dt.uint8
FP8X4 = mybir.dt.float8_e4m3fn_x4
ACT = mybir.ActivationFunctionType
ALU = mybir.AluOpType

P = 128
PACK = 4
SLOTS, PAGES, D, NQ, DV = 512, 2048, 512, 512, 512
QB = NQ // P
EB = DV // P
HALF = NQ // 2
RUN = 4
SCALE_ROWS, QUADRANT = 16, 32

KB = 1024
Q_HOME, CW_HOME, KW_HOME = 0, 8 * KB, 16 * KB
US_HOME = 24 * KB
EARLY_END = US_HOME + 32
V_HOME = 26 * KB
TH_HOME = 59 * KB
CS_HOME, LOW_HOME = 60 * KB, 62 * KB
THIRD_SPLIT = 128
ROW_FIRST, ROW_STEP = 32, 4
LAST_SPLIT = 288
LAST_GATHER_HOME = Q_HOME + 7 * KB
BANK = 2048
TH_BANK = 7
V_TURN_BANK = (1, 5, 6, 7)
OUT_BANK = (0, 4, 2, 5)
LAST_OUT_BANK = (3, 1)

FLOPS = 2 * SLOTS * NQ * (2 * D + DV)


def tile_attend_at_quest_topk_kernel(tc, qT, k_words, k_scales, c_words, c_scales, vT, th, us, offs, out):
    nc = tc.nc
    with ExitStack() as ctx:
        held = ctx.enter_context(tc.tile_pool(name="held", bufs=1))
        placed = ctx.enter_context(tc.tile_pool(name="placed", bufs=1))
        psum = ctx.enter_context(tc.psum_pool(name="psum", bufs=1))

        def quantise(codes, scales, values):
            nc.vector.quantize_mx(out=codes.bitcast(FP8X4), scales=scales, in_=values)

        q_rows = qT[0].rearrange("(p j) q -> p j q", j=PACK)
        q_raw = [held.tile([P, PACK, HALF], F32, name="q_raw0"),
                 placed.tile([P, PACK, HALF], F32, name="q_raw1", offset=Q_HOME)]
        nc.sync.dma_start(out=q_raw[0][:], in_=q_rows[:, :, 0:HALF])
        offsets = held.tile([P, SLOTS // 16], U16, name="offsets")
        nc.sync.dma_start(offsets[:], offs)

        ident = held.tile([P, P], F32, name="ident")
        th_rows = placed.tile([P, P], F32, name="th_rows", offset=TH_HOME)
        warm = held.tile([P, 1], F32, name="warm")
        cs_all = placed.tile([P, PAGES], U8, name="cs_all", offset=CS_HOME)
        ks_all = placed.tile([P, EB * 8 * KB], U8, name="ks_all", offset=V_HOME)
        planes = held.tile([P, 2 * SLOTS], U8, name="planes", align_bytes=64)
        zeros = placed.tile([P, (EARLY_END - Q_HOME) // 4], F32, name="zeros", offset=Q_HOME)
        nc.gpsimd.memset(warm[:], 0.0)
        nc.scalar.activation(out=warm[:], in_=warm[:], func=ACT.Sigmoid)
        nc.gpsimd.memset(zeros[:, 0:P], 0.0)
        nc.vector.memset(cs_all[:].bitcast(I32), 0)
        nc.vector.memset(ks_all[:, 0:PAGES].bitcast(I32), 0)
        nc.vector.tensor_copy(out=th_rows[:], in_=zeros[:, 0:P])
        nc.gpsimd.memset(ident[:], 0.0)
        nc.gpsimd.affine_select(out=ident[:], in_=ident[:], compare_op=ALU.not_equal, fill=1.0, base=0,
                                pattern=[[-1, P]], channel_multiplier=1)
        nc.gpsimd.memset(planes[:].bitcast(I32), 0)

        loaded_rows = slice(ROW_FIRST, ROW_FIRST + ROW_STEP * SCALE_ROWS, ROW_STEP)
        nc.sync.dma_start(out=cs_all[loaded_rows, :].bitcast(I32), in_=c_scales[0].bitcast(I32))
        nc.sync.dma_start(out=ks_all[loaded_rows, 0:PAGES].bitcast(I32), in_=k_scales[0].bitcast(I32))
        cw_all = placed.tile([P, PAGES], I32, name="cw_all", offset=CW_HOME)
        nc.sync.dma_start(out=cw_all[:], in_=c_words[0].rearrange("p n t -> p (n t)").bitcast(I32))
        nc.sync.dma_start(out=th_rows[0:QB, :], in_=th[0, 0].rearrange("(c p) -> c p", p=P))
        us_col = placed.tile([P, PACK], F32, name="us_col", offset=US_HOME)
        nc.sync.dma_start(out=us_col[:], in_=us[0].rearrange("(p t) o -> p (t o)", t=PACK))
        kw_all = placed.tile([P, PAGES], I32, name="kw_all", offset=KW_HOME)
        nc.sync.dma_start(out=kw_all[:], in_=k_words[0].rearrange("p n t -> p (n t)").bitcast(I32))
        nc.sync.dma_start(out=q_raw[1][:], in_=q_rows[:, :, HALF:NQ])

        rows_g = held.tile([P, 2 * SLOTS], U8, name="rows_g", align_bytes=64)
        nc.vector.tensor_copy(out=rows_g[:, 0:SLOTS], in_=cs_all[:].indirect(offsets[:]))
        nc.vector.tensor_copy(out=rows_g[:, SLOTS:2 * SLOTS], in_=ks_all[:, 0:PAGES].indirect(offsets[:]))
        for r in range(4):
            first = ROW_FIRST + ROW_STEP * r
            nc.sync.dma_start(out=planes[r:P:QUADRANT, :].bitcast(I32),
                              in_=rows_g[first:first + 4 * 4 * ROW_STEP:4 * ROW_STEP, :].bitcast(I32))
        v_all = []
        for a in range(EB):
            v_tile = placed.tile([P, PAGES], F32, name=f"v_all{a}", offset=V_HOME + a * 8 * KB)
            nc.sync.dma_start(out=v_tile[:], in_=vT[a * P:(a + 1) * P, :])
            v_all.append(v_tile)

        q_bf = [held.tile([P, HALF, PACK], BF16, name="q_bf0", align_bytes=64)]
        lo_bf = [placed.tile([P, HALF, PACK], BF16, name="lo_bf0", offset=CS_HOME, align_bytes=64),
                 held.tile([P, HALF, PACK], BF16, name="lo_bf1", align_bytes=64)]
        hi_bf = [held.tile([P, HALF, PACK], BF16, name="hi_bf0", align_bytes=64),
                 placed.tile([P, HALF, PACK], BF16, name="hi_bf1", offset=LOW_HOME, align_bytes=64)]
        lo_codes = [placed.tile([P, HALF], U32, name="lo_codes0", offset=CW_HOME, align_bytes=64),
                    held.tile([P, HALF], U32, name="lo_codes1", align_bytes=64)]
        hi_codes = [placed.tile([P, HALF], U32, name="hi_codes0", offset=CW_HOME + KB, align_bytes=64),
                    held.tile([P, HALF], U32, name="hi_codes1", align_bytes=64)]
        lo_scales = [held.tile([P, HALF], U8, name=f"lo_scales{h}", align_bytes=64) for h in range(2)]
        hi_scales = [held.tile([P, HALF], U8, name=f"hi_scales{h}", align_bytes=64) for h in range(2)]

        def round_queries(h):
            nc.scalar.copy(out=q_bf[h][:], in_=q_raw[h][:].rearrange("p j q -> p q j"))

        def quantise_queries(h):
            quantise(lo_codes[h][:], lo_scales[h][:], lo_bf[h][:].rearrange("p q j -> p (q j)"))
            quantise(hi_codes[h][:], hi_scales[h][:], hi_bf[h][:].rearrange("p q j -> p (q j)"))

        round_queries(0)
        nc.scalar.activation(out=hi_bf[0][:], in_=q_bf[0][:], func=ACT.Relu)
        nc.vector.tensor_scalar_min(out=lo_bf[0][:], in0=q_bf[0][:], scalar1=0.0)
        cw_g = held.tile([P, SLOTS], U32, name="cw_g", align_bytes=64)
        nc.vector.tensor_copy(out=cw_g[:], in_=cw_all[:].bitcast(U32).indirect(offsets[:]))
        quantise_queries(0)
        kw_g = held.tile([P, SLOTS], U32, name="kw_g", align_bytes=64)
        nc.vector.tensor_copy(out=kw_g[:], in_=kw_all[:].bitcast(U32).indirect(offsets[:]))

        th_ps = psum.tile([P, P], F32, name="th_ps", offset=TH_BANK * BANK)
        nc.tensor.transpose(th_ps[:], th_rows[:], ident[:])
        neg_th = held.tile([P, QB], F32, name="neg_th")
        nc.scalar.activation(out=neg_th[:], in_=th_ps[:, 0:QB], func=ACT.Copy, scale=-1.0)
        us_laid = held.tile([P, P, PACK], F32, name="us_laid")
        nc.scalar.copy(out=us_laid[:], in_=us_col[:].unsqueeze(1).to_broadcast([P, P, PACK]))

        second = q_raw[1][:].rearrange("p j q -> p q j")
        nc.scalar.activation(out=hi_bf[1][:], in_=second, func=ACT.Relu)
        nc.vector.tensor_scalar_min(out=lo_bf[1][:], in0=second, scalar1=0.0)
        quantise_queries(1)

        idle_ps = psum.tile([P, SLOTS], F32, name="idle_ps", offset=TH_BANK * BANK)
        for c in range(2):
            nc.tensor.matmul_mx(out=idle_ps[:], lhsT=cw_g[:, c * P:(c + 1) * P].bitcast(FP8X4),
                                lhsT_scale=rows_g[:, c * P:(c + 1) * P], rhs=cw_g[:].bitcast(FP8X4),
                                rhs_scale=rows_g[:, 0:SLOTS], start=True, stop=True)

        scores = [psum.tile([P, SLOTS], F32, name=f"score{c}", offset=c * BANK) for c in range(QB)]

        def score_pass(c, codes, scales, keys, plane, first):
            cols = slice(c % 2 * P, (c % 2 + 1) * P)
            nc.tensor.matmul_mx(out=scores[c][:], lhsT=codes[c // 2][:, cols].bitcast(FP8X4),
                                lhsT_scale=scales[c // 2][:, cols], rhs=keys[:].bitcast(FP8X4), rhs_scale=plane,
                                start=first, stop=not first)

        for c in range(QB):
            score_pass(c, lo_codes, lo_scales, cw_g, planes[:, 0:SLOTS], True)
            score_pass(c, hi_codes, hi_scales, kw_g, planes[:, SLOTS:2 * SLOTS], False)

        out_rows = out[0].rearrange("(c p) e -> p c e", p=P)
        y_bf = [placed.tile([P, HALF, PACK], BF16, name=f"y_bf{h}", offset=V_HOME + h * 2 * KB, align_bytes=64)
                for h in range(2)]
        y_codes = [held.tile([P, HALF], U32, name=f"y_codes{h}", align_bytes=64) for h in range(2)]
        y_scales = [held.tile([P, HALF], U8, name=f"y_scales{h}", align_bytes=64) for h in range(2)]
        v_g = [placed.tile([P, SLOTS], BF16, name="v_g0", offset=LOW_HOME),
               held.tile([P, SLOTS], BF16, name="v_g1"), held.tile([P, SLOTS], BF16, name="v_g2"),
               placed.tile([P, SLOTS], BF16, name="v_g3", offset=LAST_GATHER_HOME)]

        def gate(c):
            sig = held.tile([P, PACK, P], F32, name=f"sig{c}")
            nc.scalar.activation(out=sig[:], in_=scores[c][:].rearrange("q (s t) -> q t s", t=PACK),
                                 func=ACT.Sigmoid, bias=neg_th[:, c:c + 1])
            return sig

        def turn_gate(c, sig):
            turned = psum.tile([P, PACK, P], F32, name=f"y_ps{c}", offset=c * BANK)
            for t in range(PACK):
                nc.tensor.transpose(turned[:, t, :], sig[:, t, :], ident[:])
            return turned

        def scale_gate(c, turned):
            nc.vector.tensor_tensor(out=y_bf[c // 2][:, c % 2 * P:(c % 2 + 1) * P, :],
                                    in0=turned[:].rearrange("p t q -> p q t"), in1=us_laid[:], op=ALU.mult)

        def quantise_gates(h):
            quantise(y_codes[h][:], y_scales[h][:], y_bf[h][:].rearrange("p q t -> p (q t)"))

        def gather_on_vector(a, first, last):
            nc.vector.tensor_copy(out=v_g[a][:, first:last], in_=v_all[a][:].indirect(offsets[:, first // 16:last // 16]))

        def gather_on_scalar(a, first, last):
            nc.scalar.activation(out=v_g[a][:, first:last], in_=v_all[a][:].indirect(offsets[:, first // 16:last // 16]),
                                 func=ACT.Copy)

        def turn_values(a):
            pairs = v_g[a][:].bitcast(F32)
            v_ps = psum.tile([P, 2, P], F32, name=f"v_ps{a}", offset=V_TURN_BANK[a] * BANK)
            for u in range(2):
                nc.tensor.transpose(v_ps[:, u, :], pairs[:, u:SLOTS // 2:2], ident[:])
            return v_ps

        def lay_values(words, v_ps, copy):
            copy(out=words, in_=v_ps[:].rearrange("p u e -> p e u"))

        def quantise_values(name, words, home):
            width = words.shape[1]
            v_codes = placed.tile([P, width], U32, name="v_codes" + name, offset=home, align_bytes=64)
            v_scales = held.tile([P, width], U8, name="v_scales" + name, align_bytes=64)
            quantise(v_codes[:], v_scales[:], words.rearrange("p e u -> p (e u)").bitcast(BF16))
            return v_codes, v_scales

        def multiply(first, operand, blocks, bank, copy, queue, home):
            v_codes, v_scales = operand
            width = v_codes.shape[1]
            name = f"{first}_{blocks[0]}"
            acc = psum.tile([P, len(blocks), width], F32, name="out_ps" + name, offset=bank * BANK)
            for i, c in enumerate(blocks):
                cols = slice(c % 2 * P, (c % 2 + 1) * P)
                nc.tensor.matmul_mx(out=acc[:, i, :], lhsT=y_codes[c // 2][:, cols].bitcast(FP8X4),
                                    lhsT_scale=y_scales[c // 2][:, cols],
                                    rhs=v_codes[:].bitcast(FP8X4), rhs_scale=v_scales[:], start=True, stop=True)
            result = placed.tile([P, len(blocks), width], F32, name="result" + name, offset=home)
            copy(out=result[:], in_=acc[:])
            queue.dma_start(out=out_rows[:, blocks[0]:blocks[-1] + 1, first:first + width], in_=result[:])

        every_block = list(range(QB))
        sigs = [gate(c) for c in range(QB)]
        gather_on_vector(0, 0, SLOTS)
        turned = [turn_gate(c, sigs[c]) for c in range(QB)]
        for c in range(QB - 1):
            scale_gate(c, turned[c])
        quantise_gates(0)
        scale_gate(QB - 1, turned[QB - 1])
        v_words = [held.tile([P, P, 2], F32, name=f"v_words{a}", align_bytes=64) for a in range(2)]
        v_words.extend(placed.tile([P, P, 2], F32, name=f"v_words{a}", offset=V_HOME + (22 + 2 * (a - 1)) * KB, align_bytes=64)
                       for a in range(2, EB))
        quantise_gates(1)
        lay_values(v_words[0][:], turn_values(0), nc.vector.tensor_copy)
        gather_on_scalar(1, 0, SLOTS)
        v_ps1 = turn_values(1)
        operand0 = quantise_values("0", v_words[0][:], V_HOME + 8 * KB)
        lay_values(v_words[1][:], v_ps1, nc.vector.tensor_copy)
        gather_on_vector(2, 0, THIRD_SPLIT)
        gather_on_scalar(2, THIRD_SPLIT, SLOTS)
        v_ps2 = turn_values(2)
        operand1 = quantise_values("1", v_words[1][:], V_HOME + 16 * KB)
        gather_on_vector(3, 0, LAST_SPLIT)
        gather_on_scalar(3, LAST_SPLIT, SLOTS)
        v_ps3 = turn_values(3)
        lay_values(v_words[2][:], v_ps2, nc.scalar.copy)
        multiply(0, operand0, every_block, OUT_BANK[0], nc.vector.tensor_copy, nc.sync, V_HOME + 28 * KB)
        operand2 = quantise_values("2", v_words[2][:], Q_HOME + KB)
        multiply(P, operand1, every_block[:2], OUT_BANK[1], nc.scalar.copy, nc.sync, V_HOME + 30 * KB)
        lay_values(v_words[3][:], v_ps3, nc.scalar.copy)
        multiply(P, operand1, every_block[2:], V_TURN_BANK[2], nc.scalar.copy, nc.sync, LAST_GATHER_HOME)
        last = quantise_values("3", v_words[3][:], Q_HOME + 3 * KB // 2)
        multiply(2 * P, operand2, every_block[:2], OUT_BANK[2], nc.scalar.copy, nc.sync, Q_HOME + 2 * KB)
        multiply(2 * P, operand2, every_block[2:], OUT_BANK[3], nc.scalar.copy, nc.sync, Q_HOME + 3 * KB)
        multiply(3 * P, last, every_block[:2], LAST_OUT_BANK[0], nc.vector.tensor_copy, nc.sync, Q_HOME + 4 * KB)
        multiply(3 * P, last, every_block[2:], LAST_OUT_BANK[1], nc.scalar.copy, nc.scalar, Q_HOME + 6 * KB)
